import numpy as np, ml_dtypes
CORES = [10,34,74,98]
N = 4
import mx_ref
BF = ml_dtypes.bfloat16
def pick(q, e):
    c = np.concatenate([q[0].reshape(128, -1, 4), np.zeros((128, 1, 4), np.uint8)], axis=1); s = np.concatenate([q[1], np.ones((16, 1), np.uint8)], axis=1)
    return (np.ascontiguousarray(c[:, e].reshape(128, -1)), np.ascontiguousarray(s[:, e]))
def join(*qs):
    return (np.concatenate([q[0] for q in qs], axis=1), np.concatenate([q[1] for q in qs], axis=1))
def put(q, e, v):
    c, s = q[0].reshape(128, -1, 4).copy(), q[1].copy(); c[:, e] = v[0].reshape(128, -1, 4); s[:, e] = v[1]
    return (c.reshape(128, -1), s)
def pk(c, s):
    return (np.ascontiguousarray(c), mx_ref.live(s))
def emit(q):
    return q[0], q[1]
def decode(q):
    o = []
    for b in range(4):
        e = np.zeros((128, 128, 4), np.float32); e[np.arange(128), np.arange(128), b] = 1
        o.append(mx_ref.matmul(mx_ref.quantize(e.reshape(128, 512).astype(BF)), q))
    return np.stack(o, axis=2).reshape(128, -1)
def cut(t, i, w=512):
    return t[:, w * i:w * i + w]
def f(rng, *shape):
    return mx_ref.flush((rng.standard_normal(shape, dtype=np.float32) * np.exp2(rng.integers(-2, 3, shape[:-1] + (1,)))).astype(BF))
def wide(rng, *shape, cols=0):
    v = rng.standard_normal(shape, dtype=np.float32) * np.exp2(rng.integers(-12, 13, shape)).astype(np.float32)
    if cols: v *= np.repeat(np.exp2(rng.integers(-cols, cols + 1, shape[:-2] + (1, shape[-1] // 4))) * (rng.random(shape[:-2] + (1, shape[-1] // 4)) > 0.0625), 4, axis=-1).astype(np.float32)
    return mx_ref.flush(v.astype(BF))
P, K, R, O = 384, 64, 2, 1
def big(v):
    v = v.astype(np.float32)
    v[np.abs(v) < np.float32(2.0 ** -16)] = 0
    return v.astype(BF)
def plain(rng):
    u = np.array(f(rng, N, 128, 512))
    u[:, :, 4 * R:] = 0
    return {"c": big(f(rng, N, 128, 4 * P)), "u": u, "w": f(rng, N, 128, 512 * O)}
def bf(v, *shape):
    return np.ascontiguousarray(v).reshape(shape).astype(np.float32).astype(BF)
def signs(rng):
    return rng.choice([-1.0, 1.0], (128, 1, 4))
def heavy(rng, way):
    d, g = plain(rng), signs(rng)
    size = np.exp2(rng.integers(0, 3, (N, P)))
    size[np.arange(N), rng.integers(0, P, N)] = 1024
    d["c"] = bf((1 + rng.random((N, 128, P, 4))) * size[:, None, :, None] * g * 2.0 ** 18, N, 128, 4 * P)
    d["u"][:, :, :4 * R] = bf((1 + rng.random((N, 128, R, 4))) * g * np.asarray(way)[:, None] * 2.0 ** 28, N, 128, 4 * R)
    return d
def setup_inputs(rng):
    return plain(rng)
def setup_inputs_one(rng):
    return heavy(rng, np.ones(R))
def setup_inputs_chain(rng):
    return heavy(rng, np.where(np.arange(R) == 0, 1.0, -1.0))
def setup_inputs_apart(rng):
    d, g = plain(rng), signs(rng)
    v = np.zeros((N, 128, P, 4))
    for r in range(N):
        at = rng.permutation(P)
        a, b = at[:K], at[K:2 * K]
        v[r][np.arange(K), a] = 32 * (1 + rng.random((K, 4)))
        v[r][np.arange(K), b] = 32 * (1 + rng.random((K, 4)))
        v[r][64:96, a] = -(1 + 0.125 * rng.random((32, K, 4)))
        v[r][64:96, at[K:]] = 4096
        v[r][96:, at[K:]] = 1 + rng.random((32, P - K, 4))
    d["c"] = bf(v * g * 2.0 ** 18, N, 128, 4 * P)
    q = (1 + rng.random((N, 128, R, 4))) * g
    q[:, :64] = 0
    d["u"][:, :, :4 * R] = bf(q, N, 128, 4 * R)
    return d
def setup_inputs_ties(rng):
    d, g = plain(rng), signs(rng)
    v = np.abs(d["c"].astype(np.float32)).reshape(N, 128, P, 4)[:, :, :8] * g
    v[:, :, 0] = 0
    h = [rng.permutation(np.arange(P) % 8) for r in range(N)]
    for r in range(0, N, 2):
        i = int(np.flatnonzero(h[r] == 0)[0])
        h[r][i] = h[r][0]
        h[r][0] = 0
    d["c"] = bf(np.stack([v[r][:, h[r]] for r in range(N)]), N, 128, 4 * P)
    d["u"][:, :, :4] = bf(np.abs(d["u"][:, :, :4].astype(np.float32)).reshape(N, 128, 1, 4) * g, N, 128, 4)
    return d
def setup_inputs_spread(rng):
    d = plain(rng)
    d["u"][:, :, 4:8] = 0
    return {**d, "c": big(wide(rng, N, 128, 4 * P, cols=6))}
def check_inputs(d):
    b = []
    for k, low in (("c", 2.0 ** -16), ("u", 2.0 ** -30), ("w", 2.0 ** -30)):
        v = np.abs(d[k].astype(np.float32))
        if not (np.isfinite(v).all() and ((v == 0) | (v >= low) & (v <= 2.0 ** 30)).all()): b.append("a value of " + k)
    if (d["u"][:, :, 4 * R:].astype(np.float32) != 0).any(): b.append("u has numbers behind its first R columns")
    return b
def reference(c, u, w):
    tg = np.zeros((N, R, K), np.float32)
    cs = [mx_ref.quantize(np.ascontiguousarray(c[r])) for r in range(N)]
    qu = [mx_ref.quantize(np.ascontiguousarray(u[r])) for r in range(N)]
    half, zero = np.float32(0.5), np.float32(0)
    for t in range(R):
        left, sent = [], []
        for r in range(N):
            s = mx_ref.matmul(qu[r], cs[r])[t] + zero
            left.append(np.argsort(s, kind="stable")[:K])
            sent.append(pick(cs[r], left[r]))
        for r in range(N):
            a = sent[r ^ (1 << t)]
            z = mx_ref.matmul(pick(a, np.concatenate([np.arange(K), np.full(128 - K, -1)])), cs[r])[:K] + zero
            z[:, left[r]] = -np.inf
            to = np.argmax(z, axis=1)
            merge = np.sort(np.unique(to, return_index=True)[1])
            fill = np.setdiff1d(np.arange(K), merge)
            places = np.sort(left[r])[:len(fill)]
            v = decode(join(cs[r], a)).reshape(128, P + K, 4)
            v[:, to[merge]] = half * v[:, to[merge]] + half * v[:, P + merge]
            new = mx_ref.quantize(np.ascontiguousarray(v[:, :P]).reshape(128, -1).astype(BF))
            q = put(cs[r], to[merge], pick(new, to[merge]))
            cs[r] = put(q, places, pick(a, fill))
            tg[r, t, merge] = to[merge]
            tg[r, t, fill] = -1 - places
    oc, osc, y = np.zeros((N, 128, 4 * P), np.uint8), np.zeros((N, 16, P), np.uint8), np.zeros((N, 128, O * P), np.float32)
    for r in range(N):
        oc[r], osc[r] = emit(cs[r])
        for o in range(O):
            y[r, :, o * P:o * P + P] = mx_ref.matmul(mx_ref.quantize(np.ascontiguousarray(cut(w[r], o))), cs[r])
    return {"oc": oc, "osc": osc, "tg": tg, "y": y}

@@ -1,0 +1,410 @@
+from concourse.mybir import dt, AluOpType as A, AxisListType, ActivationFunctionType as F
+
+F8, U8, BF, F32, U16 = "float8_e4m3fn_x4", "uint8", "bfloat16", "float32", "uint16"
+C16 = 12582912.0
+C32 = 402653184.0
+SCRATCH = {"ps": ("psum", [128, 4096], F32)}
+for _t, _l in (
+        (BF, "ct 1536 u8 8 ut 1024 wt 512 modb 128 lli 128 one 512 eb 520 w16 512 trs 512 whl 1024 tri 128 idn 128 "
+             "neg 384 m8 8 cm 68 kb 24 mk 1152 scn 576 xl 512 x1 512 xs 1536 cum 384 pre 64 jk 385 jk2 384 xt 512 "
+             "eq 64 xab 608 mt 512"),
+        (F32, "uf 8 pj 128 p1 1 k24 24 jb 4 h4 4 l4 4 jd 24 jd1 24 jh 24 yy 1 p16 1 pr1 1 g64 1 bc 1 sc 3 sd 3 th 384 "
+              "tt 128 lv 3 n0 1 n1 1 e3 24 zr 388 ix 1 tc 1 t1 1 hh 1 ll 1 fb 1 qa 1 hd 1 md 1 mc 1 h16 1 m16 1 vv 1 "
+              "sg 1 so 1 y1 1 qf 1 q16 1 r1 1 de 1 dh 1 dl 1 tgs 2 ysb 384"),
+        (U16, "ofl 4 ofr 24 oft 4 ofs 24"),
+        (F8, "uq 256 wq 128 kq 1152 xlq 128 x1q 128 xsq 384 xtq 128 xfq 128 abq 152 c0 384 c1 384 c2 384 "
+             "win0 576 win1 576 rep0 384 rep1 384 snd0 64 snd1 64"),
+        (U8, "us 256 ws 128 ks 1152 xls 128 x1s 128 xss 384 xts 128 xfs 128 abp 152 cs0 384 cs1 384 cs2 384 "
+             "wins0 576 wins1 576 reps0 384 reps1 384 snds0 64 snds1 64")):
+    _w = _l.split()
+    for _n, _c in zip(_w[::2], _w[1::2]):
+        SCRATCH[_n] = ("sbuf", [128, int(_c)], _t)
+NDMA = 24
+SEMAPHORES = ["sv", "ss", "st", "sp", "loc", "arr0", "arr1"] + ["d%d" % i for i in range(NDMA)]
+ONES, W16, TRS, WH, WL, EB = 0, 128, 256, 384, 512, 640
+
+
+def rank_program(g, core, T, topo):
+    rank = T.rank_of(core)
+    if rank is None:
+        return
+    queue = {"v": g.vector, "s": g.scalar, "t": g.tensor, "p": g, "y": g.sync}
+    own = {"v": "sv", "s": "ss", "t": "st", "p": "sp"}
+    count = {s: 0 for s in SEMAPHORES}
+    clock = {}
+    known = {q: {} for q in queue}
+    hist = {}
+    ndma = [0]
+
+    def merge(a, b):
+        for s, v in b.items():
+            if a.get(s, 0) < v:
+                a[s] = v
+
+    def dep(q, rd, wr):
+        need = {}
+        for lst, w in ((rd, False), (wr, True)):
+            for reg in lst:
+                name, lo, hi = reg[0], reg[1], reg[2]
+                st = reg[3] if len(reg) > 3 else 1
+                psum = name == "ps"
+                if psum:
+                    lo, hi, st = lo // 512 * 512, (hi + 511) // 512 * 512, 1
+                for (l2, h2, s2, q2, w2, sem, val) in hist.get(name, ()):
+                    if l2 >= hi or lo >= h2 or (st == s2 and st > 1 and (lo - l2) % st):
+                        continue
+                    if psum and q == q2 and (q == "t" or not (w or w2)):
+                        continue
+                    if w or w2 or (psum and q != q2):
+                        need[sem] = max(need.get(sem, 0), val)
+        for sem in sorted(need, key=lambda s: s == own.get(q)):
+            if known[q].get(sem, 0) < need[sem]:
+                queue[q].wait_ge(T.sem[sem], need[sem])
+                merge(known[q], clock[(sem, need[sem])])
+
+    def note(q, rd, wr, sem, val):
+        c = dict(known[q])
+        c[sem] = val
+        if (sem, val - 1) in clock:
+            merge(c, clock[(sem, val - 1)])
+        clock[(sem, val)] = c
+        for lst, w in ((rd, False), (wr, True)):
+            for reg in lst:
+                name, lo, hi = reg[0], reg[1], reg[2]
+                st = reg[3] if len(reg) > 3 else 1
+                if name == "ps":
+                    lo, hi, st = lo // 512 * 512, (hi + 511) // 512 * 512, 1
+                hist.setdefault(name, []).append((lo, hi, st, q, w, sem, val))
+
+    def view(reg):
+        name, lo, hi = reg[0], reg[1], reg[2]
+        return T[name][:, lo:hi:reg[3]] if len(reg) > 3 else T[name][:, lo:hi]
+
+    def run(q, call, rd, wr):
+        dep(q, rd, wr)
+        sem = own[q]
+        count[sem] += 1
+        call().then_inc(T.sem[sem], 1)
+        note(q, rd, wr, sem, count[sem])
+
+    def whole(name):
+        return (name, 0, SCRATCH[name][1][1])
+
+    def R(x):
+        return whole(x) if isinstance(x, str) else x
+
+    def isreg(x):
+        return isinstance(x, (str, tuple))
+
+    def memset(o, v):
+        o = R(o)
+        run("v", lambda: g.vector.memset(view(o), v), [], [o])
+
+    def ts(o, i, s1, op0, s2=None, op1=None):
+        o, i = R(o), R(i)
+        rd = [i] + [R(s) for s in (s1, s2) if isreg(s)]
+        a = view(R(s1)) if isreg(s1) else s1
+        b = view(R(s2)) if isreg(s2) else s2
+        if op1 is None:
+            run("v", lambda: g.vector.tensor_scalar(view(o), view(i), a, None, op0), rd, [o])
+        else:
+            run("v", lambda: g.vector.tensor_scalar(view(o), view(i), a, b, op0, op1), rd, [o])
+
+    def tt(o, a, b, op):
+        o, a, b = R(o), R(a), R(b)
+        run("v", lambda: g.vector.tensor_tensor(view(o), view(a), view(b), op), [a, b], [o])
+
+    def cp(o, i):
+        o, i = R(o), R(i)
+        run("v", lambda: g.vector.tensor_copy(view(o), view(i)), [i], [o])
+
+    def red(o, i, op):
+        o, i = R(o), R(i)
+        run("v", lambda: g.vector.tensor_reduce(view(o), view(i), AxisListType.X, op), [i], [o])
+
+    def scan(o, a, b, init, op0, op1):
+        o, a, b = R(o), R(a), R(b)
+        run("v", lambda: g.vector.tensor_tensor_scan(view(o), view(a), view(b), init, op0, op1), [a, b], [o])
+
+    def act(o, i, func, bias=None, scale=None, acc=None):
+        o, i = R(o), R(i)
+        rd, wr, kw = [i], [o], {}
+        for k, x in (("bias", bias), ("scale", scale)):
+            if isreg(x):
+                rd.append(R(x))
+                kw[k] = view(R(x))
+            elif x is not None:
+                kw[k] = x
+        if acc is not None:
+            wr.append(R(acc))
+            kw["accum_out"] = view(R(acc))
+        run("s", lambda: g.scalar.activation(view(o), view(i), func, **kw), rd, wr)
+
+    def quant(qn, sn, lo, n, src, slo):
+        s = (src, slo, slo + 4 * n)
+        run("v", lambda: g.vector.quantize_mx(T[qn][:, lo:lo + n], T[sn][:, lo:lo + n], view(s)),
+            [s], [(qn, lo, lo + n), (sn, lo, lo + n)])
+
+    def mm(bank, n, l, r, start=True, stop=True):
+        o = ("ps", 512 * bank, 512 * bank + n)
+        rl = [(l[0], l[2], l[2] + 128), (l[1], l[2], l[2] + 128), (r[0], r[2], r[2] + n), (r[1], r[2], r[2] + n)]
+        run("t", lambda: g.tensor.matmul_mx(view(o), view(rl[0]), view(rl[1]), view(rl[2]), view(rl[3]), start, stop),
+            rl, [o])
+
+    def pick(o, os, olo, n, win, wins, width, off, off0):
+        k = (off, off0, off0 + n // 16)
+        run("v", lambda: g.vector.tensor_copy(T[o][:, olo:olo + n].bitcast(dt.uint32),
+                                              T[win][:, 0:width].bitcast(dt.uint32).indirect(view(k))),
+            [(win, 0, width), k], [(o, olo, olo + n)])
+        run("s", lambda: g.scalar.activation(T[os][:, olo:olo + n], T[wins][:, 0:width].indirect(view(k)), F.Copy),
+            [(wins, 0, width), k], [(os, olo, olo + n)])
+
+    def iota(o, pattern, base, cm):
+        o = R(o)
+        run("p", lambda: g.iota(view(o), pattern, base, cm, allow_small_or_imprecise_dtypes=True), [], [o])
+
+    def dma(q, out, in_, rd, wr):
+        dep(q, rd, wr)
+        sem = "d%d" % ndma[0]
+        ndma[0] += 1
+        count[sem] = 16
+        queue[q].dma_start(out, in_).then_inc(T.sem[sem], 16)
+        note(q, rd, wr, sem, 16)
+
+    K = ("kq", "ks")
+
+    dma("y", T.u8[:], T.u[:, 0:8], [], [whole("u8")])
+    dma("s", T.ct[:, 0:512], T.c[:, 0:512], [], [("ct", 0, 512)])
+    dma("y", T.ct[:, 512:1024], T.c[:, 512:1024], [], [("ct", 512, 1024)])
+    dma("s", T.ct[:, 1024:1536], T.c[:, 1024:1536], [], [("ct", 1024, 1536)])
+
+    iota("jb", [[128, 4]], 0, 1)
+    iota("p1", [[0, 1]], 1, 1)
+    iota("pj", [[1, 128]], 0, -1)
+    iota("lli", [[16, 4], [0, 2], [1, 16]], 0, 0)
+    iota("modb", [[0, 8], [1, 16]], 1, 0)
+    iota("k24", [[1, 24]], 0, 0)
+    for name in ("eb", "x1", "xt"):
+        iota(name, [[0, SCRATCH[name][1][1]]], 0, 0)
+    iota(("mt", 256, 512), [[0, 256]], 0, 0)
+    memset("one", 1.0)
+    ts("h4", "jb", C32, A.add, C32, A.subtract)
+    tt("l4", "jb", "h4", A.subtract)
+    for h, x in ((0, "h4"), (1, "l4")):
+        for b in range(4):
+            act(("whl", 512 * h + b, 512 * h + 512, 4), ("one", 0, 128), F.Copy, scale=(x, b, b + 1))
+    act(("xl", 3, 512, 4), ("one", 0, 128), F.Copy, scale=0.0)
+    quant(*K, ONES, 128, "one", 0)
+    ts("tri", "pj", 0.0, A.is_lt)
+    ts("yy", "p1", -8.5, A.add, 0.0625, A.mult)
+    ts("p16", "yy", C16, A.add, C16, A.subtract)
+    ts("pr1", "p16", -16.0, A.mult, "p1", A.add)
+    ts("idn", "pj", 0.0, A.is_equal)
+    ts(("w16", 0, 512, 4), "modb", "pr1", A.is_equal)
+    ts(("trs", 0, 512, 4), "pj", 0.0, A.is_gt)
+    memset("neg", -1e29)
+    for e in range(4):
+        ts(("ut", e, 512, 4), ("one", 0, 128), ("u8", e, e + 1), A.mult)
+    quant("uq", "us", 0, 128, "ut", 0)
+    quant(*K, WH, 256, "whl", 0)
+
+    def scores(t, b):
+        c, s, u = "c%d" % t, "cs%d" % t, ("uq", "us", 128 * t)
+        mm(b, 128, (c, s, 128 * b), u)
+        mm(3 + b, 128, u, (c, s, 128 * b))
+
+    def thresholds(b):
+        act(("sc", b, b + 1), ("ps", 512 * b, 512 * b + 1), F.Copy)
+        act(("sd", b, b + 1), ("sc", b, b + 1), F.Abs, bias=2.0 ** -120, scale=0.6 * 2.0 ** -23)
+        act(("th", 128 * b, 128 * b + 128), "tri", F.Identity, bias=("sc", b, b + 1), scale=("sd", b, b + 1))
+
+    for b in range(3):
+        quant("c0", "cs0", 128 * b, 128, "ct", 512 * b)
+        scores(0, b)
+        thresholds(b)
+    for x in ("w16", "trs"):
+        for i in range(3):
+            act((x, i + 1, 512, 4), (x, 0, 512, 4), F.Copy)
+    act(("eb", 4, 516, 4), "idn", F.Copy, scale=0.5)
+    for i in range(2):
+        act(("xs", 512 * i, 512 * i + 512), "one", F.Copy, scale=0.0)
+    ts("jd1", "k24", 16.0, A.mult, "pr1", A.add)
+    ts("m8", ("k24", 0, 8), "p16", A.is_equal, -512.0, A.mult)
+    ts("jd", "jd1", -1.0, A.add)
+    ts(("cm", 0, 64), ("pj", 0, 64), 0.0, A.is_equal)
+    ts(("cm", 64, 68), ("k24", 0, 4), "p16", A.is_equal)
+    ts("g64", "p1", 65.0, A.is_ge, -1000.0, A.mult)
+    ts("bc", "p1", 384.0, A.add)
+    ts("kb", "k24", "g64", A.add)
+
+    for t in range(2):
+        c, cs, win, wins = "c%d" % t, "cs%d" % t, "win%d" % t, "wins%d" % t
+        rep, reps, snd, snds = "rep%d" % t, "reps%d" % t, "snd%d" % t, "snds%d" % t
+        nc, ncs = "c%d" % (t + 1), "cs%d" % (t + 1)
+        dma("y", T[win][:, 64:448].bitcast(dt.uint8), T[c][:, 0:384].bitcast(dt.uint8), [whole(c)], [(win, 64, 448)])
+        dma("y", T[wins][:, 64:448], T[cs][:, 0:384], [whole(cs)], [(wins, 64, 448)])
+
+        def against(b, d):
+            o, i = ("mk", 384 * b + 128 * d, 384 * b + 128 * d + 128), ("ps", 512 * (3 + d), 512 * (3 + d) + 128)
+            if b == d:
+                tt(o, i, ("th", 128 * b, 128 * b + 128), A.is_lt)
+            else:
+                ts(o, i, ("sc", b, b + 1), A.is_le if d < b else A.is_lt)
+
+        def total(b):
+            scan(("scn", 192 * b, 192 * b + 192), ("mk", 384 * b, 384 * b + 192), ("mk", 384 * b + 192, 384 * b + 384),
+                 0.0, A.add, A.add)
+
+        def onehot(b):
+            ts(("xl", b, 512, 4), "lli", ("scn", 192 * b + 191, 192 * b + 192), A.is_equal)
+
+        for b, d in ((0, 1), (1, 0), (0, 0), (1, 1), (0, 2), (1, 2)):
+            against(b, d)
+        total(0)
+        against(2, 0)
+        total(1)
+        against(2, 1)
+        onehot(0)
+        against(2, 2)
+        onehot(1)
+        total(2)
+        onehot(2)
+        quant("xlq", "xls", 0, 128, "xl", 0)
+        mm(6, 128, K + (WH,), ("xlq", "xls", 0), True, False)
+        mm(6, 128, K + (WL,), ("xlq", "xls", 0), False, True)
+        if t == 0:
+            quant(*K, W16, 128, "w16", 0)
+            quant(*K, TRS, 128, "trs", 0)
+        ts("lv", ("scn", 191, 576, 192), 64.0, A.is_lt)
+        run("v", lambda: g.vector.transpose(T.tt[:], T.ps[:, 3072:3200]), [("ps", 3072, 3200)], [whole("tt")])
+        cp("ofl", ("tt", 0, 128, 32))
+        pick(snd, snds, 0, 64, c, cs, 384, "ofl", 0)
+        dst = T.cores[rank ^ (1 << t)]
+        rid, pid, _ = topo.addr(dst)
+        m = topo.mask(core, dst)
+        ne = len(topo.engines(core, dst))
+        arr = "arr%d" % t
+        for o, s in ((win, snd), (wins, snds)):
+            dep("p", [whole(s)], [])
+            w, i = T[o][:, 0:64], T[s][:, 0:64]
+            if o == win:
+                w, i = w.bitcast(dt.uint8), i.bitcast(dt.uint8)
+            g.remote_dma(w, i, T.sem[arr], T.sem["loc"], pid, rid, m)
+            count["loc"] += ne
+        count[arr] = 2 * ne
+        clock[(arr, 2 * ne)] = {arr: 2 * ne}
+        for o in (win, wins):
+            hist.setdefault(o, []).append((0, 64, 1, "-", True, arr, 2 * ne))
+        if t == 0:
+            act(("xs", 1024, 1536), "one", F.Copy, scale=0.0)
+        ts(("x1", 0, 256, 4), "idn" if False else ("idn", 0, 64), ("lv", 0, 1), A.mult)
+        for b in range(3):
+            ts(("x1", 256 + 32 * b, 288 + 32 * b, 4), "m8", ("lv", b, b + 1), A.mult)
+        quant("x1q", "x1s", 0, 128, "x1", 0)
+        mm(7, 128, K + (ONES,), ("x1q", "x1s", 0))
+        mm(0, 128, K + (W16,), ("x1q", "x1s", 0))
+        for b in range(3):
+            ts(("xs", 512 * b, 512 * b + 512, 4), "idn", ("lv", b, b + 1), A.mult)
+        scan("pre", ("ps", 3584, 3648), ("neg", 0, 64), 1.0, A.mult, A.max)
+        red("n0", "pre", A.add)
+        tt("e3", ("ps", 64, 88), "jd", A.add)
+        ts("ofr", "e3", "n0", A.max)
+        pick(rep, reps, 0, 384, c, cs, 384, "ofr", 0)
+        ts("n1", "n0", 1.0, A.add)
+        quant("xsq", "xss", 0, 384, "xs", 0)
+        mm(7, 384, K + (ONES,), ("xsq", "xss", 0))
+        if t == 0:
+            memset(("zr", 3, 4), -1e29)
+            cp("uf", "u8")
+            for e in range(4):
+                act(("ut", 512 + e, 1024, 4), ("one", 0, 128), F.Copy, scale=("uf", 4 + e, 5 + e))
+            for e in (2, 3):
+                ts(("xab", 96 + e, 608, 4), "modb", "p1", A.is_equal)
+            ts("jd1", "jd", 64.0, A.add)
+            ts("jh", "jd1", C32, A.add, C32, A.subtract)
+            cp(("xab", 2, 96, 4), "jh")
+            tt(("xab", 3, 96, 4), "jd1", "jh", A.subtract)
+            dma("y", T.wt[:], T.w[:], [], [whole("wt")])
+            for b in range(4):
+                quant(*K, EB + 128 * b, 128, "eb", 4 - b)
+        else:
+            quant("wq", "ws", 0, 128, "wt", 0)
+        mm(1, 384, (win, wins, 0), (rep, reps, 0))
+        for b in range(4):
+            mm(2 + b, 128, K + (EB + 128 * b,), (win, wins, 0), True, False)
+        scan(("zr", 4, 388), ("ps", 512, 896), "neg", -1e29, A.max, A.max)
+        act("jk", ("zr", 3, 388), F.Sign, bias=("zr", 387, 388), scale=-1.0, acc="ix")
+        scan("cum", ("ps", 3584, 3968), "neg", 0.0, A.add, A.max)
+        ts("tc", "ix", "n1", A.max, C32, A.add)
+        ts("t1", "ix", "n1", A.max)
+        ts("hh", "tc", C32, A.subtract)
+        ts("ll", "tc", C32, A.subtract, "t1", A.subtract)
+        ts(("xt", 0, 272, 4), "cm", "hh", A.mult)
+        ts(("xt", 1, 272, 4), "cm", "ll", A.mult, -1.0, A.mult)
+        quant("xtq", "xts", 0, 128, "xt", 0)
+        mm(6, 128, K + (TRS,), ("xtq", "xts", 0))
+        mm(7, 128, K + (W16,), ("xtq", "xts", 0))
+        if t == 0:
+            quant("uq", "us", 128, 128, "ut", 512)
+        dup = ("xt", 400, 401)
+        ts("eq", ("ps", 3072, 3136), "t1", A.is_equal)
+        red(dup, "eq", A.max)
+        quant("xfq", "xfs", 0, 128, "xt", 0)
+        mm(0, 128, K + (TRS,), ("xfq", "xfs", 0))
+        ts("oft", ("ps", 3648, 3652), -1.0, A.add)
+        pick(rep, reps, 0, 64, c, cs, 384, "oft", 0)
+        act("fb", ("ps", 100, 101), F.Identity, bias=0.5)
+        act("jk2", "cum", F.Sign, bias="fb", scale=-1.0, acc="qa")
+        for b in range(4):
+            mm(2 + b, 128, K + (EB + 128 * b,), (rep, reps, 0), False, True)
+        ts("md", "t1", -193.0, A.add, dup, A.mult)
+        ts("h16", dup, 0.03125, A.mult)
+        ts("hd", dup, 0.5, A.mult)
+        tt("mc", "t1", "md", A.subtract)
+        ts("vv", dup, -448.0, A.mult, "bc", A.add)
+        ts("m16", "mc", -8.5, A.add, 0.0625, A.mult)
+        ts("sg", dup, -2.0, A.mult, 1.0, A.add)
+        ts("so", dup, -1.0, A.add)
+        for b in range(4):
+            act(("mt", b, 256, 4), ("ps", 512 * (2 + b), 512 * (2 + b) + 64), F.Copy)
+        ts("y1", "qa", "h16", A.mult, "m16", A.add)
+        ts("qf", "qa", "hd", A.mult, "mc", A.add)
+        ts("q16", "y1", C16, A.add, C16, A.subtract)
+        tt("de", "vv", "qf", A.subtract)
+        ts("r1", "q16", -16.0, A.mult, "qf", A.add)
+        ts("dh", "de", C32, A.add, C32, A.subtract)
+        ts(("xab", 96, 608, 4), "modb", "r1", A.is_equal)
+        tt("dl", "de", "dh", A.subtract)
+        ts(("xab", 97, 608, 4), "modb", "r1", A.is_equal)
+        ts(("xab", 0, 96, 4), "kb", "q16", A.is_equal, "dh", A.mult)
+        ts(("xab", 1, 96, 4), "kb", "q16", A.is_equal, "dl", A.mult)
+        quant("abq", "abp", 0, 152, "xab", 0)
+        mm(1, 128, ("abq", "abp", 24), ("abq", "abp", 0))
+        quant(win, wins, 448, 128, "mt", 0)
+        cp("ofs", ("ps", 512, 536))
+        for b in range(3):
+            pick(nc, ncs, 128 * b, 128, win, wins, 512, "ofs", 8 * b)
+            if t == 0:
+                scores(1, b)
+            else:
+                mm((6, 7, 0)[b], 128, ("wq", "ws", 0), (nc, ncs, 128 * b))
+                dma("y", T.oc[:, 512 * b:512 * b + 512], T[nc][:, 128 * b:128 * b + 128].bitcast(dt.uint8),
+                    [(nc, 128 * b, 128 * b + 128)], [])
+        if t == 0:
+            ts(("tgs", 0, 1), "qf", "sg", A.mult, "so", A.add)
+            for b in range(3):
+                thresholds(b)
+            dma("y", T.tg[0, :], T.tgs[0:64, 0:1], [("tgs", 0, 1)], [])
+        else:
+            for k in range(4):
+                dma("ys"[k // 2], T.osc[4 * k:4 * k + 4, :], T[ncs][32 * k:32 * k + 4, 0:384], [whole(ncs)], [])
+            ts(("tgs", 1, 2), "qf", "sg", A.mult, "so", A.add)
+            for b in range(2):
+                cp(("ysb", 128 * b, 128 * b + 128), ("ps", 512 * (6 + b), 512 * (6 + b) + 128))
+            act(("ysb", 256, 384), ("ps", 0, 128), F.Copy)
+            dma("y", T.y[:, 0:256], T.ysb[:, 0:256], [("ysb", 0, 256)], [])
+            dma("s", T.y[:, 256:384], T.ysb[:, 256:384], [("ysb", 256, 384)], [])
+            dma("y", T.tg[1, :], T.tgs[0:64, 1:2], [("tgs", 1, 2)], [])
+    for s in SEMAPHORES:
+        if count[s]:
+            g.wait_ge(T.sem[s], count[s])

@@ -6,11 +6,11 @@ C32 = 402653184.0
 SCRATCH = {"ps": ("psum", [128, 4096], F32)}
 for _t, _l in (
         (BF, "ct 1536 u8 8 ut 1024 wt 512 modb 128 lli 128 one 512 eb 520 w16 512 trs 512 whl 1024 tri 128 idn 128 "
-             "neg 384 m8 8 cm 68 kb 24 mk 1152 scn 576 xl 512 x1 512 xs 1536 cum 384 pre 64 jk 385 jk2 384 xt 512 "
-             "eq 64 xab 608 mt 512"),
-        (F32, "uf 8 pj 128 p1 1 k24 24 jb 4 h4 4 l4 4 jd 24 jd1 24 jh 24 yy 1 p16 1 pr1 1 g64 1 bc 1 sc 3 sd 3 th 384 "
-              "tt 128 lv 3 n0 1 n1 1 e3 24 zr 388 ix 1 tc 1 t1 1 hh 1 ll 1 fb 1 qa 1 hd 1 md 1 mc 1 h16 1 m16 1 vv 1 "
-              "sg 1 so 1 y1 1 qf 1 q16 1 r1 1 de 1 dh 1 dl 1 tgs 2 ysb 384"),
+             "neg 384 m8 8 cm 68 kb 24 mk 1152 scn 576 xl 512 x1 512 xs 1536 cum 384 pre 64 cap 384 jk 385 jk2 384 "
+             "xt 512 e12 12 e24 24 eq 64 xab 608 mt 512"),
+        (F32, "uf 8 pj 128 p1 1 k24 24 jb 4 h4 4 l4 4 jd 24 jd1 24 yy 1 p16 1 pr1 1 g64 1 bc 1 hb 1 sc 3 sd 3 th 384 "
+              "tt 128 lv 3 n0 1 e3 24 zr 388 ix 1 i32 1 ww 1 ll 1 fb 1 qa 1 mc 1 nd 1 me 1 vh 1 vl 1 "
+              "sg 1 so 1 y1 1 t16 1 tu 1 qe 1 qf 1 z16 1 src 24 tgs 2 ysb 384"),
         (U16, "ofl 4 ofr 24 oft 4 ofs 24"),
         (F8, "uq 256 wq 128 kq 1152 xlq 128 x1q 128 xsq 384 xtq 128 xfq 128 abq 152 c0 384 c1 384 c2 384 "
              "win0 576 win1 576 rep0 384 rep1 384 snd0 64 snd1 64"),
@@ -19,7 +19,7 @@ for _t, _l in (
     _w = _l.split()
     for _n, _c in zip(_w[::2], _w[1::2]):
         SCRATCH[_n] = ("sbuf", [128, int(_c)], _t)
-NDMA = 24
+NDMA = 26
 SEMAPHORES = ["sv", "ss", "st", "sp", "loc", "arr0", "arr1"] + ["d%d" % i for i in range(NDMA)]
 ONES, W16, TRS, WH, WL, EB = 0, 128, 256, 384, 512, 640
 
@@ -202,47 +202,62 @@ def rank_program(g, core, T, topo):
     ts("idn", "pj", 0.0, A.is_equal)
     ts(("w16", 0, 512, 4), "modb", "pr1", A.is_equal)
     ts(("trs", 0, 512, 4), "pj", 0.0, A.is_gt)
-    memset("neg", -1e29)
     for e in range(4):
         ts(("ut", e, 512, 4), ("one", 0, 128), ("u8", e, e + 1), A.mult)
     quant("uq", "us", 0, 128, "ut", 0)
-    quant(*K, WH, 256, "whl", 0)
 
     def scores(t, b):
         c, s, u = "c%d" % t, "cs%d" % t, ("uq", "us", 128 * t)
         mm(b, 128, (c, s, 128 * b), u)
         mm(3 + b, 128, u, (c, s, 128 * b))
 
-    def thresholds(b):
+    def column(b):
         act(("sc", b, b + 1), ("ps", 512 * b, 512 * b + 1), F.Copy)
-        act(("sd", b, b + 1), ("sc", b, b + 1), F.Abs, bias=2.0 ** -120, scale=0.6 * 2.0 ** -23)
+
+    def threshold(b):
+        act(("sd", b, b + 1), ("ps", 512 * b, 512 * b + 1), F.Abs, bias=2.0 ** -120, scale=0.6 * 2.0 ** -23)
         act(("th", 128 * b, 128 * b + 128), "tri", F.Identity, bias=("sc", b, b + 1), scale=("sd", b, b + 1))
 
     for b in range(3):
         quant("c0", "cs0", 128 * b, 128, "ct", 512 * b)
         scores(0, b)
-        thresholds(b)
-    for x in ("w16", "trs"):
-        for i in range(3):
-            act((x, i + 1, 512, 4), (x, 0, 512, 4), F.Copy)
-    act(("eb", 4, 516, 4), "idn", F.Copy, scale=0.5)
-    for i in range(2):
-        act(("xs", 512 * i, 512 * i + 512), "one", F.Copy, scale=0.0)
+    quant(*K, WH, 256, "whl", 0)
     ts("jd1", "k24", 16.0, A.mult, "pr1", A.add)
     ts("m8", ("k24", 0, 8), "p16", A.is_equal, -512.0, A.mult)
     ts("jd", "jd1", -1.0, A.add)
-    ts(("cm", 0, 64), ("pj", 0, 64), 0.0, A.is_equal)
-    ts(("cm", 64, 68), ("k24", 0, 4), "p16", A.is_equal)
-    ts("g64", "p1", 65.0, A.is_ge, -1000.0, A.mult)
-    ts("bc", "p1", 384.0, A.add)
-    ts("kb", "k24", "g64", A.add)
+
+    def early():
+        for x in ("w16", "trs"):
+            for i in range(3):
+                act((x, i + 1, 512, 4), (x, 0, 512, 4), F.Copy)
+        act(("eb", 4, 516, 4), "idn", F.Copy, scale=0.5)
+        act("neg", ("one", 0, 384), F.Copy, scale=-1e29)
+        act(("xs", 0, 512), "one", F.Copy, scale=0.0)
+
+    def later():
+        ts(("cm", 0, 64), ("pj", 0, 64), 0.0, A.is_equal)
+        ts(("cm", 64, 68), ("k24", 0, 4), "p16", A.is_equal)
+        ts("g64", "p1", 65.0, A.is_ge, -1000.0, A.mult)
+        ts("bc", "p1", 447.0, A.add)
+        ts("kb", "k24", 16.0, A.mult, "g64", A.add)
+        ts("hb", "bc", C32, A.add, C32, A.subtract)
+        tt("vl", "bc", "hb", A.subtract)
+
+    dup = ("xt", 400, 401)
+
+    def outcome(r):
+        ts("sg", dup, -4.0, A.mult, 1.0, A.add)
+        ts("so", "nd", -1.0, A.mult)
+        ts(("tgs", r, r + 1), "qf", "sg", A.mult, "so", A.add)
 
     for t in range(2):
         c, cs, win, wins = "c%d" % t, "cs%d" % t, "win%d" % t, "wins%d" % t
         rep, reps, snd, snds = "rep%d" % t, "reps%d" % t, "snd%d" % t, "snds%d" % t
         nc, ncs = "c%d" % (t + 1), "cs%d" % (t + 1)
-        dma("y", T[win][:, 64:448].bitcast(dt.uint8), T[c][:, 0:384].bitcast(dt.uint8), [whole(c)], [(win, 64, 448)])
-        dma("y", T[wins][:, 64:448], T[cs][:, 0:384], [whole(cs)], [(wins, 64, 448)])
+        dma("y", T[win][:, 0:384].bitcast(dt.uint8), T[c][:, 0:384].bitcast(dt.uint8), [whole(c)], [(win, 0, 384)])
+        dma("y", T[wins][:, 0:384], T[cs][:, 0:384], [whole(cs)], [(wins, 0, 384)])
+        dma("y", T[win][:, 448:512].bitcast(dt.uint8), T[c][:, 0:64].bitcast(dt.uint8), [(c, 0, 64)], [(win, 448, 512)])
+        dma("y", T[wins][:, 448:512], T[cs][:, 0:64], [(cs, 0, 64)], [(wins, 448, 512)])
 
         def against(b, d):
             o, i = ("mk", 384 * b + 128 * d, 384 * b + 128 * d + 128), ("ps", 512 * (3 + d), 512 * (3 + d) + 128)
@@ -258,7 +273,15 @@ def rank_program(g, core, T, topo):
         def onehot(b):
             ts(("xl", b, 512, 4), "lli", ("scn", 192 * b + 191, 192 * b + 192), A.is_equal)
 
-        for b, d in ((0, 1), (1, 0), (0, 0), (1, 1), (0, 2), (1, 2)):
+        column(0)
+        column(1)
+        threshold(0)
+        threshold(1)
+        column(2)
+        threshold(2)
+        if t == 0:
+            early()
+        for b, d in ((0, 1), (1, 0), (0, 2), (1, 2), (0, 0), (1, 1)):
             against(b, d)
         total(0)
         against(2, 0)
@@ -286,7 +309,7 @@ def rank_program(g, core, T, topo):
         arr = "arr%d" % t
         for o, s in ((win, snd), (wins, snds)):
             dep("p", [whole(s)], [])
-            w, i = T[o][:, 0:64], T[s][:, 0:64]
+            w, i = T[o][:, 384:448], T[s][:, 0:64]
             if o == win:
                 w, i = w.bitcast(dt.uint8), i.bitcast(dt.uint8)
             g.remote_dma(w, i, T.sem[arr], T.sem["loc"], pid, rid, m)
@@ -294,23 +317,27 @@ def rank_program(g, core, T, topo):
         count[arr] = 2 * ne
         clock[(arr, 2 * ne)] = {arr: 2 * ne}
         for o in (win, wins):
-            hist.setdefault(o, []).append((0, 64, 1, "-", True, arr, 2 * ne))
+            hist.setdefault(o, []).append((384, 448, 1, "-", True, arr, 2 * ne))
         if t == 0:
-            act(("xs", 1024, 1536), "one", F.Copy, scale=0.0)
-        ts(("x1", 0, 256, 4), "idn" if False else ("idn", 0, 64), ("lv", 0, 1), A.mult)
+            for i in (1, 2):
+                act(("xs", 512 * i, 512 * i + 512), "one", F.Copy, scale=0.0)
+            act(("cap", 64, 384), ("one", 0, 320), F.Copy, scale=1e29)
+        ts(("x1", 0, 256, 4), ("idn", 0, 64), ("lv", 0, 1), A.mult)
         for b in range(3):
             ts(("x1", 256 + 32 * b, 288 + 32 * b, 4), "m8", ("lv", b, b + 1), A.mult)
         quant("x1q", "x1s", 0, 128, "x1", 0)
         mm(7, 128, K + (ONES,), ("x1q", "x1s", 0))
         mm(0, 128, K + (W16,), ("x1q", "x1s", 0))
-        for b in range(3):
-            ts(("xs", 512 * b, 512 * b + 512, 4), "idn", ("lv", b, b + 1), A.mult)
+        if t == 0:
+            later()
         scan("pre", ("ps", 3584, 3648), ("neg", 0, 64), 1.0, A.mult, A.max)
         red("n0", "pre", A.add)
         tt("e3", ("ps", 64, 88), "jd", A.add)
         ts("ofr", "e3", "n0", A.max)
         pick(rep, reps, 0, 384, c, cs, 384, "ofr", 0)
-        ts("n1", "n0", 1.0, A.add)
+        ts(("cap", 0, 64), "pre", -2e29, A.mult, 1e29, A.add)
+        for b in range(3):
+            ts(("xs", 512 * b, 512 * b + 512, 4), "idn", ("lv", b, b + 1), A.mult, 0.5, A.mult)
         quant("xsq", "xss", 0, 384, "xs", 0)
         mm(7, 384, K + (ONES,), ("xsq", "xss", 0))
         if t == 0:
@@ -318,70 +345,66 @@ def rank_program(g, core, T, topo):
             cp("uf", "u8")
             for e in range(4):
                 act(("ut", 512 + e, 1024, 4), ("one", 0, 128), F.Copy, scale=("uf", 4 + e, 5 + e))
-            for e in (2, 3):
-                ts(("xab", 96 + e, 608, 4), "modb", "p1", A.is_equal)
-            ts("jd1", "jd", 64.0, A.add)
-            ts("jh", "jd1", C32, A.add, C32, A.subtract)
-            cp(("xab", 2, 96, 4), "jh")
-            tt(("xab", 3, 96, 4), "jd1", "jh", A.subtract)
+            act(("xab", 0, 512), "one", F.Copy, scale=0.0)
+            act(("xab", 512, 608), ("one", 0, 96), F.Copy, scale=0.0)
+            ts(("xt", 2, 272, 4), "cm", 16.0, A.mult)
             dma("y", T.wt[:], T.w[:], [], [whole("wt")])
             for b in range(4):
                 quant(*K, EB + 128 * b, 128, "eb", 4 - b)
         else:
             quant("wq", "ws", 0, 128, "wt", 0)
-        mm(1, 384, (win, wins, 0), (rep, reps, 0))
+            outcome(0)
+            dma("y", T.tg[0, :], T.tgs[0:64, 0:1], [("tgs", 0, 1)], [])
+        mm(1, 384, (win, wins, 384), (rep, reps, 0))
         for b in range(4):
-            mm(2 + b, 128, K + (EB + 128 * b,), (win, wins, 0), True, False)
-        scan(("zr", 4, 388), ("ps", 512, 896), "neg", -1e29, A.max, A.max)
-        act("jk", ("zr", 3, 388), F.Sign, bias=("zr", 387, 388), scale=-1.0, acc="ix")
+            mm(2 + b, 128, K + (EB + 128 * b,), (win, wins, 384), True, False)
         scan("cum", ("ps", 3584, 3968), "neg", 0.0, A.add, A.max)
-        ts("tc", "ix", "n1", A.max, C32, A.add)
-        ts("t1", "ix", "n1", A.max)
-        ts("hh", "tc", C32, A.subtract)
-        ts("ll", "tc", C32, A.subtract, "t1", A.subtract)
-        ts(("xt", 0, 272, 4), "cm", "hh", A.mult)
-        ts(("xt", 1, 272, 4), "cm", "ll", A.mult, -1.0, A.mult)
+        scan(("zr", 4, 388), ("ps", 512, 896), "cap", -1e29, A.max, A.min)
+        act("jk", ("zr", 3, 388), F.Sign, bias=("zr", 387, 388), scale=-1.0, acc="ix")
+        ts("e12", ("zr", 35, 388, 32), ("zr", 387, 388), A.is_lt)
+        red("i32", "e12", A.add)
+        ts(("xt", 0, 272, 4), "cm", "i32", A.mult, 32.0, A.mult)
+        ts("ww", "i32", 32.0, A.mult, 16.0, A.add)
+        tt("ll", "ix", "ww", A.subtract)
+        ts(("xt", 1, 272, 4), "cm", "ll", A.mult)
         quant("xtq", "xts", 0, 128, "xt", 0)
         mm(6, 128, K + (TRS,), ("xtq", "xts", 0))
         mm(7, 128, K + (W16,), ("xtq", "xts", 0))
+        ts("y1", "ix", -8.5, A.add)
+        ts("tu", "ix", -193.0, A.add)
+        ts("t16", "y1", 16.0 * C16, A.add, 16.0 * C16, A.subtract)
         if t == 0:
             quant("uq", "us", 128, 128, "ut", 512)
-        dup = ("xt", 400, 401)
-        ts("eq", ("ps", 3072, 3136), "t1", A.is_equal)
+        ts("eq", ("ps", 3072, 3136), "ix", A.is_equal, 0.5, A.mult)
         red(dup, "eq", A.max)
         quant("xfq", "xfs", 0, 128, "xt", 0)
         mm(0, 128, K + (TRS,), ("xfq", "xfs", 0))
+        mm(6, 128, K + (TRS,), ("xfq", "xfs", 0))
+        ts("nd", dup, -2.0, A.mult, 1.0, A.add)
         ts("oft", ("ps", 3648, 3652), -1.0, A.add)
         pick(rep, reps, 0, 64, c, cs, 384, "oft", 0)
-        act("fb", ("ps", 100, 101), F.Identity, bias=0.5)
+        act("fb", ("ps", 100, 101), F.Identity, bias=0.25)
         act("jk2", "cum", F.Sign, bias="fb", scale=-1.0, acc="qa")
         for b in range(4):
             mm(2 + b, 128, K + (EB + 128 * b,), (rep, reps, 0), False, True)
-        ts("md", "t1", -193.0, A.add, dup, A.mult)
-        ts("h16", dup, 0.03125, A.mult)
-        ts("hd", dup, 0.5, A.mult)
-        tt("mc", "t1", "md", A.subtract)
-        ts("vv", dup, -448.0, A.mult, "bc", A.add)
-        ts("m16", "mc", -8.5, A.add, 0.0625, A.mult)
-        ts("sg", dup, -2.0, A.mult, 1.0, A.add)
-        ts("so", dup, -1.0, A.add)
+        ts("me", "t16", "nd", A.mult)
+        ts("vh", dup, -128.0, A.mult, "hb", A.add)
+        ts("mc", "tu", "nd", A.mult, 193.0, A.add)
         for b in range(4):
             act(("mt", b, 256, 4), ("ps", 512 * (2 + b), 512 * (2 + b) + 64), F.Copy)
-        ts("y1", "qa", "h16", A.mult, "m16", A.add)
-        ts("qf", "qa", "hd", A.mult, "mc", A.add)
-        ts("q16", "y1", C16, A.add, C16, A.subtract)
-        tt("de", "vv", "qf", A.subtract)
-        ts("r1", "q16", -16.0, A.mult, "qf", A.add)
-        ts("dh", "de", C32, A.add, C32, A.subtract)
-        ts(("xab", 96, 608, 4), "modb", "r1", A.is_equal)
-        tt("dl", "de", "dh", A.subtract)
-        ts(("xab", 97, 608, 4), "modb", "r1", A.is_equal)
-        ts(("xab", 0, 96, 4), "kb", "q16", A.is_equal, "dh", A.mult)
-        ts(("xab", 1, 96, 4), "kb", "q16", A.is_equal, "dl", A.mult)
+        ts("e24", ("cum", 15, 384, 16), ("ps", 3172, 3173), A.is_le, 32.0, A.mult)
+        red("qe", "e24", A.add)
+        ts("z16", dup, "qe", A.mult, "me", A.add)
+        ts("qf", dup, "qa", A.mult, "mc", A.add)
+        ts(("xab", 0, 96, 4), "kb", "z16", A.is_equal, "vh", A.mult)
+        ts(("xab", 96, 608, 4), "modb", "z16", A.add, "qf", A.is_equal)
+        ts(("xab", 97, 608, 4), "modb", "z16", A.add, "qf", A.is_equal)
+        ts(("xab", 1, 96, 4), "kb", "z16", A.is_equal, "vl", A.mult)
         quant("abq", "abp", 0, 152, "xab", 0)
         mm(1, 128, ("abq", "abp", 24), ("abq", "abp", 0))
         quant(win, wins, 448, 128, "mt", 0)
-        cp("ofs", ("ps", 512, 536))
+        tt("src", ("ps", 512, 536), "jd", A.max)
+        cp("ofs", "src")
         for b in range(3):
             pick(nc, ncs, 128 * b, 128, win, wins, 512, "ofs", 8 * b)
             if t == 0:
@@ -390,18 +413,13 @@ def rank_program(g, core, T, topo):
                 mm((6, 7, 0)[b], 128, ("wq", "ws", 0), (nc, ncs, 128 * b))
                 dma("y", T.oc[:, 512 * b:512 * b + 512], T[nc][:, 128 * b:128 * b + 128].bitcast(dt.uint8),
                     [(nc, 128 * b, 128 * b + 128)], [])
-        if t == 0:
-            ts(("tgs", 0, 1), "qf", "sg", A.mult, "so", A.add)
-            for b in range(3):
-                thresholds(b)
-            dma("y", T.tg[0, :], T.tgs[0:64, 0:1], [("tgs", 0, 1)], [])
-        else:
+        if t == 1:
             for k in range(4):
                 dma("ys"[k // 2], T.osc[4 * k:4 * k + 4, :], T[ncs][32 * k:32 * k + 4, 0:384], [whole(ncs)], [])
-            ts(("tgs", 1, 2), "qf", "sg", A.mult, "so", A.add)
-            for b in range(2):
-                cp(("ysb", 128 * b, 128 * b + 128), ("ps", 512 * (6 + b), 512 * (6 + b) + 128))
+            cp(("ysb", 0, 128), ("ps", 3072, 3200))
+            cp(("ysb", 128, 256), ("ps", 3584, 3712))
             act(("ysb", 256, 384), ("ps", 0, 128), F.Copy)
+            outcome(1)
             dma("y", T.y[:, 0:256], T.ysb[:, 0:256], [("ysb", 0, 256)], [])
             dma("s", T.y[:, 256:384], T.ysb[:, 256:384], [("ysb", 256, 384)], [])
             dma("y", T.tg[1, :], T.tgs[0:64, 1:2], [("tgs", 1, 2)], [])

@@ -5,23 +5,23 @@ C16 = 12582912.0
 C32 = 402653184.0
 SCRATCH = {"ps": ("psum", [128, 4096], F32)}
 for _t, _l in (
-        (BF, "ct 1536 u8 8 ut 1024 wt 512 modb 128 lli 128 one 512 eb 520 w16 512 trs 512 whl 1024 tri 128 idn 128 "
-             "neg 384 m8 8 cm 68 kb 24 mk 1152 scn 576 xl 512 x1 512 xs 1536 cum 384 pre 64 cap 384 jk 385 jk2 384 "
-             "xt 512 e12 12 e24 24 eq 64 xab 608 mt 512"),
-        (F32, "uf 8 pj 128 p1 1 k24 24 jb 4 h4 4 l4 4 jd 24 jd1 24 yy 1 p16 1 pr1 1 g64 1 bc 1 hb 1 sc 3 sd 3 th 384 "
-              "tt 128 lv 3 n0 1 e3 24 zr 388 ix 1 i32 1 ww 1 ll 1 fb 1 qa 1 mc 1 nd 1 me 1 vh 1 vl 1 "
-              "sg 1 so 1 y1 1 t16 1 tu 1 qe 1 qf 1 z16 1 src 24 tgs 2 ysb 384"),
+        (BF, "ct 1536 u8 8 ut 1024 wt 512 modb 128 mo2 256 mf2 256 lli 128 one 512 eb 520 w16 512 trs 512 whl 1024 "
+             "tri 128 idn 128 ngt 512 m8 8 cm 72 kb 24 kf 24 kr 64 mk 1152 scn 576 xl 512 x1 512 xk 512 cap 384 jk 385 "
+             "xt 512 e12 12 e0 1 xab 608 mt 512"),
+        (F32, "uf 8 pj 128 p1 1 k24 24 jb 4 h4 4 l4 4 jd 24 jd1 1 yy 1 p16 1 pr1 1 g64 1 bc 1 hb 1 vl 1 sc 3 sd 3 "
+              "th 384 tt 128 lv 3 lvs 3 n0 1 kh 64 zr 388 ix 1 i32 1 ww 1 ll 1 y1 1 t16 1 nhf 1 hf 1 nvl 1 vhm 1 vlm 1 "
+              "vhf 1 vlf 1 tab 128 tmp 64 xx 128 pl 1 ph 1 so 1 sg 1 src 24 tgs 2 ysb 384"),
         (U16, "ofl 4 ofr 24 oft 4 ofs 24"),
-        (F8, "uq 256 wq 128 kq 1152 xlq 128 x1q 128 xsq 384 xtq 128 xfq 128 abq 152 c0 384 c1 384 c2 384 "
+        (F8, "uq 256 wq 128 kq 1280 xlq 128 x1q 128 xkq 128 xtq 128 xfq 128 abq 152 c0 384 c1 384 c2 384 "
              "win0 576 win1 576 rep0 384 rep1 384 snd0 64 snd1 64"),
-        (U8, "us 256 ws 128 ks 1152 xls 128 x1s 128 xss 384 xts 128 xfs 128 abp 152 cs0 384 cs1 384 cs2 384 "
+        (U8, "us 256 ws 128 ks 1280 xls 128 x1s 128 xks 128 xts 128 xfs 128 abp 152 cs0 384 cs1 384 cs2 384 "
              "wins0 576 wins1 576 reps0 384 reps1 384 snds0 64 snds1 64")):
     _w = _l.split()
     for _n, _c in zip(_w[::2], _w[1::2]):
         SCRATCH[_n] = ("sbuf", [128, int(_c)], _t)
 NDMA = 26
 SEMAPHORES = ["sv", "ss", "st", "sp", "loc", "arr0", "arr1"] + ["d%d" % i for i in range(NDMA)]
-ONES, W16, TRS, WH, WL, EB = 0, 128, 256, 384, 512, 640
+ONES, W16, TRS, WH, WL, EB, NEG = 0, 128, 256, 384, 512, 640, 1152
 
 
 def rank_program(g, core, T, topo):
@@ -35,6 +35,7 @@ def rank_program(g, core, T, topo):
     known = {q: {} for q in queue}
     hist = {}
     ndma = [0]
+    part = [False]
 
     def merge(a, b):
         for s, v in b.items():
@@ -122,6 +123,11 @@ def rank_program(g, core, T, topo):
         o, i = R(o), R(i)
         run("v", lambda: g.vector.tensor_reduce(view(o), view(i), AxisListType.X, op), [i], [o])
 
+    def least(o, i):
+        o, i = R(o), R(i)
+        run("v", lambda: g.vector.tensor_reduce(view(o), view(i), AxisListType.X, A.min, apply_absolute_value=True),
+            [i], [o])
+
     def scan(o, a, b, init, op0, op1):
         o, a, b = R(o), R(a), R(b)
         run("v", lambda: g.vector.tensor_tensor_scan(view(o), view(a), view(b), init, op0, op1), [a, b], [o])
@@ -159,9 +165,15 @@ def rank_program(g, core, T, topo):
         run("s", lambda: g.scalar.activation(T[os][:, olo:olo + n], T[wins][:, 0:width].indirect(view(k)), F.Copy),
             [(wins, 0, width), k], [(os, olo, olo + n)])
 
-    def iota(o, pattern, base, cm):
+    def iota(o, pattern, base, cm, p0=0, p1=128):
         o = R(o)
-        run("p", lambda: g.iota(view(o), pattern, base, cm, allow_small_or_imprecise_dtypes=True), [], [o])
+        st = o[3] if len(o) > 3 else 1
+        if part[0] or p1 - p0 < 128:
+            g.wait_ge(T.sem["sp"], count["sp"])
+            merge(known["p"], clock[("sp", count["sp"])])
+        part[0] = p1 - p0 < 128
+        run("p", lambda: g.iota(T[o[0]][p0:p1, o[1]:o[2]:st], pattern, base, cm, allow_small_or_imprecise_dtypes=True),
+            [], [o])
 
     def dma(q, out, in_, rd, wr):
         dep(q, rd, wr)
@@ -184,22 +196,34 @@ def rank_program(g, core, T, topo):
     iota("lli", [[16, 4], [0, 2], [1, 16]], 0, 0)
     iota("modb", [[0, 8], [1, 16]], 1, 0)
     iota("k24", [[1, 24]], 0, 0)
-    for name in ("eb", "x1", "xt"):
-        iota(name, [[0, SCRATCH[name][1][1]]], 0, 0)
-    iota(("mt", 256, 512), [[0, 256]], 0, 0)
+    iota("x1", [[0, 512]], 0, 0)
+    iota(("x1", 1, 320, 4), [[16, 5], [0, 16]], 0, 0, 0, 1)
+    iota(("x1", 2, 320, 4), [[0, 5], [1, 16]], 0, 0, 0, 1)
+    iota(("x1", 385, 480, 4), [[0, 24]], 0, 1, 0, 16)
+    iota(("x1", 385, 448, 4), [[16, 16]], 0, 0, 32, 48)
+    iota(("x1", 449, 480, 4), [[0, 8]], 240, 0, 32, 48)
+    iota(("x1", 449, 480, 4), [[16, 8]], 16, 0, 64, 80)
+    iota("kr", [[1, 64]], 0, 0)
+    iota(("ngt", 0, 256), [[0, 256]], -1, 0)
+    iota("e0", [[0, 1]], 1, -1)
     memset("one", 1.0)
+    memset("eb", 0.0)
+    memset(("ngt", 256, 512), 0.0)
     ts("h4", "jb", C32, A.add, C32, A.subtract)
     tt("l4", "jb", "h4", A.subtract)
     for h, x in ((0, "h4"), (1, "l4")):
         for b in range(4):
             act(("whl", 512 * h + b, 512 * h + 512, 4), ("one", 0, 128), F.Copy, scale=(x, b, b + 1))
     act(("xl", 3, 512, 4), ("one", 0, 128), F.Copy, scale=0.0)
+    act("xt", "one", F.Copy, scale=0.0)
+    act("xk", "one", F.Copy, scale=0.0)
     quant(*K, ONES, 128, "one", 0)
     ts("tri", "pj", 0.0, A.is_lt)
     ts("yy", "p1", -8.5, A.add, 0.0625, A.mult)
     ts("p16", "yy", C16, A.add, C16, A.subtract)
     ts("pr1", "p16", -16.0, A.mult, "p1", A.add)
     ts("idn", "pj", 0.0, A.is_equal)
+    ts(("eb", 4, 516, 4), "pj", 0.0, A.is_equal, 0.5, A.mult)
     ts(("w16", 0, 512, 4), "modb", "pr1", A.is_equal)
     ts(("trs", 0, 512, 4), "pj", 0.0, A.is_gt)
     for e in range(4):
@@ -222,33 +246,48 @@ def rank_program(g, core, T, topo):
         quant("c0", "cs0", 128 * b, 128, "ct", 512 * b)
         scores(0, b)
     quant(*K, WH, 256, "whl", 0)
-    ts("jd1", "k24", 16.0, A.mult, "pr1", A.add)
     ts("m8", ("k24", 0, 8), "p16", A.is_equal, -512.0, A.mult)
-    ts("jd", "jd1", -1.0, A.add)
 
-    def early():
-        for x in ("w16", "trs"):
-            for i in range(3):
-                act((x, i + 1, 512, 4), (x, 0, 512, 4), F.Copy)
-        act(("eb", 4, 516, 4), "idn", F.Copy, scale=0.5)
-        act("neg", ("one", 0, 384), F.Copy, scale=-1e29)
-        act(("xs", 0, 512), "one", F.Copy, scale=0.0)
+    def constants_ranks():
+        for i in range(3):
+            act(("w16", i + 1, 512, 4), ("w16", 0, 512, 4), F.Copy)
+        for i in range(2):
+            act(("trs", i + 1, 512, 4), ("trs", 0, 512, 4), F.Copy)
+        act(("trs", 3, 512, 4), ("one", 0, 128), F.Copy)
 
-    def later():
-        ts(("cm", 0, 64), ("pj", 0, 64), 0.0, A.is_equal)
-        ts(("cm", 64, 68), ("k24", 0, 4), "p16", A.is_equal)
-        ts("g64", "p1", 65.0, A.is_ge, -1000.0, A.mult)
+    def constants_sent():
+        iota("mo2", [[0, 8], [1, 16], [0, 2]], 1, 0)
+        iota(("mt", 256, 512), [[0, 256]], 0, 0)
+        act("kh", "kr", F.Copy, bias=0.5)
+        act(("cap", 64, 384), ("one", 0, 320), F.Copy, scale=1e29)
+
+    def constants_travel():
+        act(("cm", 0, 64), ("idn", 0, 64), F.Copy)
+        act(("cm", 64, 68), ("one", 0, 4), F.Copy, scale=0.0)
+        act("jd1", "pr1", F.Copy, bias=-1.0)
+        act(("xt", 259, 260), "e0", F.Relu)
+        act("uf", "u8", F.Copy)
+        act("jd", "k24", F.Identity, scale=16.0, bias="jd1")
+        for e in range(4):
+            act(("ut", 512 + e, 1024, 4), ("one", 0, 128), F.Copy, scale=("uf", 4 + e, 5 + e))
+        ts(("cm", 68, 72), ("k24", 0, 4), "p16", A.is_equal)
+        memset(("zr", 3, 4), -1e29)
         ts("bc", "p1", 447.0, A.add)
-        ts("kb", "k24", 16.0, A.mult, "g64", A.add)
+        ts("g64", "p1", 65.0, A.is_ge, -1000.0, A.mult)
         ts("hb", "bc", C32, A.add, C32, A.subtract)
-        tt("vl", "bc", "hb", A.subtract)
+        quant(*K, NEG, 128, "ngt", 0)
+        act(("xt", 2, 288, 4), "cm", F.Copy, scale=16.0)
 
-    dup = ("xt", 400, 401)
+    def constants_lists():
+        act("vl", "hb", F.Identity, scale=-1.0, bias="bc")
+        act("hf", "hb", F.Copy, bias=-64.0)
+        act("kb", "k24", F.Identity, scale=16.0, bias="g64")
+        act("kf", "k24", F.Identity, scale=1.0 / 64, bias="g64")
+        act("nhf", "hb", F.Copy, scale=-1.0, bias=64.0)
+        act("nvl", "vl", F.Copy, scale=-1.0)
+        act("mf2", "mo2", F.Copy, bias=-1.0 / 1024, scale=1.0 / 1024)
 
-    def outcome(r):
-        ts("sg", dup, -4.0, A.mult, 1.0, A.add)
-        ts("so", "nd", -1.0, A.mult)
-        ts(("tgs", r, r + 1), "qf", "sg", A.mult, "so", A.add)
+    nd = ("xt", 400, 401)
 
     for t in range(2):
         c, cs, win, wins = "c%d" % t, "cs%d" % t, "win%d" % t, "wins%d" % t
@@ -276,17 +315,18 @@ def rank_program(g, core, T, topo):
         column(0)
         column(1)
         threshold(0)
-        threshold(1)
         column(2)
+        threshold(1)
         threshold(2)
         if t == 0:
-            early()
-        for b, d in ((0, 1), (1, 0), (0, 2), (1, 2), (0, 0), (1, 1)):
+            constants_ranks()
+        for b, d in ((0, 1), (1, 0), (0, 2), (1, 2), (0, 0)):
             against(b, d)
         total(0)
         against(2, 0)
-        total(1)
         against(2, 1)
+        against(1, 1)
+        total(1)
         onehot(0)
         against(2, 2)
         onehot(1)
@@ -295,10 +335,14 @@ def rank_program(g, core, T, topo):
         quant("xlq", "xls", 0, 128, "xl", 0)
         mm(6, 128, K + (WH,), ("xlq", "xls", 0), True, False)
         mm(6, 128, K + (WL,), ("xlq", "xls", 0), False, True)
-        if t == 0:
-            quant(*K, W16, 128, "w16", 0)
-            quant(*K, TRS, 128, "trs", 0)
-        ts("lv", ("scn", 191, 576, 192), 64.0, A.is_lt)
+        ranks = ("scn", 191, 576, 192)
+        ts("lv", ranks, 64.0, A.is_lt)
+        for b in range(3):
+            act(("x1", 384 + 32 * b, 416 + 32 * b, 4), "m8", F.Copy, scale=("lv", b, b + 1))
+        ts(("x1", 320, 332, 4), ranks, 64.0, A.is_lt)
+        act(("x1", 327, 328), ("lv", 0, 1), F.Copy)
+        act(("x1", 331, 332), ("lv", 0, 1), F.Identity, bias=("lv", 1, 2))
+        ts(("x1", 0, 256, 4), ("idn", 0, 64), ("lv", 0, 1), A.mult, 512.0, A.mult)
         run("v", lambda: g.vector.transpose(T.tt[:], T.ps[:, 3072:3200]), [("ps", 3072, 3200)], [whole("tt")])
         cp("ofl", ("tt", 0, 128, 32))
         pick(snd, snds, 0, 64, c, cs, 384, "ofl", 0)
@@ -318,93 +362,98 @@ def rank_program(g, core, T, topo):
         clock[(arr, 2 * ne)] = {arr: 2 * ne}
         for o in (win, wins):
             hist.setdefault(o, []).append((384, 448, 1, "-", True, arr, 2 * ne))
-        if t == 0:
-            for i in (1, 2):
-                act(("xs", 512 * i, 512 * i + 512), "one", F.Copy, scale=0.0)
-            act(("cap", 64, 384), ("one", 0, 320), F.Copy, scale=1e29)
-        ts(("x1", 0, 256, 4), ("idn", 0, 64), ("lv", 0, 1), A.mult)
-        for b in range(3):
-            ts(("x1", 256 + 32 * b, 288 + 32 * b, 4), "m8", ("lv", b, b + 1), A.mult)
         quant("x1q", "x1s", 0, 128, "x1", 0)
+        if t == 0:
+            quant(*K, W16, 128, "w16", 0)
+            constants_sent()
+        act("lvs", "lv", F.Copy, scale=1.0 / 1024)
         mm(7, 128, K + (ONES,), ("x1q", "x1s", 0))
         mm(0, 128, K + (W16,), ("x1q", "x1s", 0))
-        if t == 0:
-            later()
-        scan("pre", ("ps", 3584, 3648), ("neg", 0, 64), 1.0, A.mult, A.max)
-        red("n0", "pre", A.add)
-        tt("e3", ("ps", 64, 88), "jd", A.add)
-        ts("ofr", "e3", "n0", A.max)
+        red("n0", ("ps", 3584, 3649), A.min)
+        ts("ofr", ("ps", 96, 120), "n0", A.max)
         pick(rep, reps, 0, 384, c, cs, 384, "ofr", 0)
-        ts(("cap", 0, 64), "pre", -2e29, A.mult, 1e29, A.add)
-        for b in range(3):
-            ts(("xs", 512 * b, 512 * b + 512, 4), "idn", ("lv", b, b + 1), A.mult, 0.5, A.mult)
-        quant("xsq", "xss", 0, 384, "xs", 0)
-        mm(7, 384, K + (ONES,), ("xsq", "xss", 0))
         if t == 0:
-            memset(("zr", 3, 4), -1e29)
-            cp("uf", "u8")
-            for e in range(4):
-                act(("ut", 512 + e, 1024, 4), ("one", 0, 128), F.Copy, scale=("uf", 4 + e, 5 + e))
-            act(("xab", 0, 512), "one", F.Copy, scale=0.0)
-            act(("xab", 512, 608), ("one", 0, 96), F.Copy, scale=0.0)
-            ts(("xt", 2, 272, 4), "cm", 16.0, A.mult)
+            quant(*K, TRS, 128, "trs", 0)
+        mm(6, 128, K + (TRS,), ("x1q", "x1s", 0))
+        ts(("cap", 0, 64), "kh", "n0", A.subtract, 1e27, A.mult)
+        if t == 0:
+            constants_travel()
             dma("y", T.wt[:], T.w[:], [], [whole("wt")])
-            for b in range(4):
-                quant(*K, EB + 128 * b, 128, "eb", 4 - b)
-        else:
-            quant("wq", "ws", 0, 128, "wt", 0)
-            outcome(0)
-            dma("y", T.tg[0, :], T.tgs[0:64, 0:1], [("tgs", 0, 1)], [])
         mm(1, 384, (win, wins, 384), (rep, reps, 0))
-        for b in range(4):
+        for b in range(3):
+            ts(("xk", b, 256, 4), "kr", ("ps", 3152 + b, 3153 + b), A.is_equal, ("lvs", b, b + 1), A.mult)
+        quant("xkq", "xks", 0, 128, "xk", 0)
+        mm(0, 128, K + (WH,), ("xkq", "xks", 0), True, False)
+        mm(0, 128, K + (WL,), ("xkq", "xks", 0), False, True)
+
+        def arrived(b):
+            if t == 0:
+                quant(*K, EB + 128 * b, 128, "eb", 4 - b)
             mm(2 + b, 128, K + (EB + 128 * b,), (win, wins, 384), True, False)
-        scan("cum", ("ps", 3584, 3968), "neg", 0.0, A.add, A.max)
+
+        if t == 1:
+            for b in range(4):
+                arrived(b)
         scan(("zr", 4, 388), ("ps", 512, 896), "cap", -1e29, A.max, A.min)
         act("jk", ("zr", 3, 388), F.Sign, bias=("zr", 387, 388), scale=-1.0, acc="ix")
         ts("e12", ("zr", 35, 388, 32), ("zr", 387, 388), A.is_lt)
         red("i32", "e12", A.add)
-        ts(("xt", 0, 272, 4), "cm", "i32", A.mult, 32.0, A.mult)
-        ts("ww", "i32", 32.0, A.mult, 16.0, A.add)
-        tt("ll", "ix", "ww", A.subtract)
-        ts(("xt", 1, 272, 4), "cm", "ll", A.mult)
-        quant("xtq", "xts", 0, 128, "xt", 0)
-        mm(6, 128, K + (TRS,), ("xtq", "xts", 0))
-        mm(7, 128, K + (W16,), ("xtq", "xts", 0))
-        ts("y1", "ix", -8.5, A.add)
-        ts("tu", "ix", -193.0, A.add)
-        ts("t16", "y1", 16.0 * C16, A.add, 16.0 * C16, A.subtract)
         if t == 0:
-            quant("uq", "us", 128, 128, "ut", 512)
-        ts("eq", ("ps", 3072, 3136), "ix", A.is_equal, 0.5, A.mult)
-        red(dup, "eq", A.max)
+            constants_lists()
+        ts(("xt", 0, 288, 4), "cm", "i32", A.mult, 32.0, A.mult)
+        ts("ww", "i32", 32.0, A.mult, 16.0, A.add)
+        tt(("tab", 0, 64), ("ps", 0, 64), ("pj", 0, 64), A.add)
+        act("tmp", ("tab", 0, 64), F.Copy, bias=-7.5 / 1024)
+        if t == 0:
+            arrived(0)
+        tt("ll", "ix", "ww", A.subtract)
+        ts("y1", "ix", -8.5, A.add)
+        ts(("xt", 1, 288, 4), "cm", "ll", A.mult)
+        ts("t16", "y1", 16.0 * C16, A.add, 16.0 * C16, A.subtract)
+        quant("xtq", "xts", 0, 128, "xt", 0)
+        mm(6, 128, K + (TRS,), ("xtq", "xts", 0), True, False)
+        mm(6, 128, ("xtq", "xts", 0), K + (NEG,), False, True)
+        mm(7, 128, K + (W16,), ("xtq", "xts", 0))
+        if t == 0:
+            arrived(1)
+            arrived(2)
+        else:
+            quant("wq", "ws", 0, 128, "wt", 0)
+        ts(("xab", 96, 608, 2), "mo2", "t16", A.add, "ix", A.is_equal)
+        least(nd, ("ps", 3072, 3137))
+        ts("oft", ("ps", 3652, 3656), -1.0, A.add)
         quant("xfq", "xfs", 0, 128, "xt", 0)
-        mm(0, 128, K + (TRS,), ("xfq", "xfs", 0))
         mm(6, 128, K + (TRS,), ("xfq", "xfs", 0))
-        ts("nd", dup, -2.0, A.mult, 1.0, A.add)
-        ts("oft", ("ps", 3648, 3652), -1.0, A.add)
+        if t == 0:
+            arrived(3)
+        act("vhm", nd, F.Copy, scale="hb")
+        act("vlm", nd, F.Copy, scale="vl")
         pick(rep, reps, 0, 64, c, cs, 384, "oft", 0)
-        act("fb", ("ps", 100, 101), F.Identity, bias=0.25)
-        act("jk2", "cum", F.Sign, bias="fb", scale=-1.0, acc="qa")
+        act("vhf", nd, F.Identity, scale="nhf", bias="hf")
+        act("vlf", nd, F.Identity, scale="nvl", bias="vl")
         for b in range(4):
             mm(2 + b, 128, K + (EB + 128 * b,), (rep, reps, 0), False, True)
-        ts("me", "t16", "nd", A.mult)
-        ts("vh", dup, -128.0, A.mult, "hb", A.add)
-        ts("mc", "tu", "nd", A.mult, 193.0, A.add)
         for b in range(4):
             act(("mt", b, 256, 4), ("ps", 512 * (2 + b), 512 * (2 + b) + 64), F.Copy)
-        ts("e24", ("cum", 15, 384, 16), ("ps", 3172, 3173), A.is_le, 32.0, A.mult)
-        red("qe", "e24", A.add)
-        ts("z16", dup, "qe", A.mult, "me", A.add)
-        ts("qf", dup, "qa", A.mult, "mc", A.add)
-        ts(("xab", 0, 96, 4), "kb", "z16", A.is_equal, "vh", A.mult)
-        ts(("xab", 96, 608, 4), "modb", "z16", A.add, "qf", A.is_equal)
-        ts(("xab", 97, 608, 4), "modb", "z16", A.add, "qf", A.is_equal)
-        ts(("xab", 1, 96, 4), "kb", "z16", A.is_equal, "vl", A.mult)
+        ts(("xab", 0, 96, 4), "kb", "t16", A.is_equal, "vhm", A.mult)
+        ts(("xab", 2, 96, 4), "kb", "t16", A.is_equal, "vlm", A.mult)
+        ts(("tab", 64, 128), "tmp", C16 / 64, A.add, C16 / 64, A.subtract)
+        ts("xx", "tab", ("ps", 3172, 3173), A.add)
+        least("ph", ("xx", 64, 128))
+        least("pl", ("xx", 0, 64))
+        ts(("xab", 1, 96, 4), "kf", "ph", A.is_equal, "vhf", A.mult)
+        ts(("xab", 3, 96, 4), "kf", "ph", A.is_equal, "vlf", A.mult)
+        ts(("xab", 97, 608, 2), "mf2", "ph", A.add, "pl", A.is_equal)
         quant("abq", "abp", 0, 152, "xab", 0)
         mm(1, 128, ("abq", "abp", 24), ("abq", "abp", 0))
         quant(win, wins, 448, 128, "mt", 0)
+        act("so", "pl", F.Copy, scale=-1024.0, bias=-1.0)
+        ts("sg", "ix", -1.0, A.add, "so", A.subtract)
+        if t == 0:
+            quant("uq", "us", 128, 128, "ut", 512)
         tt("src", ("ps", 512, 536), "jd", A.max)
         cp("ofs", "src")
+        ts(("tgs", t, t + 1), nd, "sg", A.mult, "so", A.add)
         for b in range(3):
             pick(nc, ncs, 128 * b, 128, win, wins, 512, "ofs", 8 * b)
             if t == 0:
@@ -413,16 +462,16 @@ def rank_program(g, core, T, topo):
                 mm((6, 7, 0)[b], 128, ("wq", "ws", 0), (nc, ncs, 128 * b))
                 dma("y", T.oc[:, 512 * b:512 * b + 512], T[nc][:, 128 * b:128 * b + 128].bitcast(dt.uint8),
                     [(nc, 128 * b, 128 * b + 128)], [])
+            if b == 0:
+                dma("y", T.tg[t, :], T.tgs[0:64, t:t + 1], [("tgs", t, t + 1)], [])
         if t == 1:
             for k in range(4):
                 dma("ys"[k // 2], T.osc[4 * k:4 * k + 4, :], T[ncs][32 * k:32 * k + 4, 0:384], [whole(ncs)], [])
             cp(("ysb", 0, 128), ("ps", 3072, 3200))
             cp(("ysb", 128, 256), ("ps", 3584, 3712))
             act(("ysb", 256, 384), ("ps", 0, 128), F.Copy)
-            outcome(1)
             dma("y", T.y[:, 0:256], T.ysb[:, 0:256], [("ysb", 0, 256)], [])
             dma("s", T.y[:, 256:384], T.ysb[:, 256:384], [("ysb", 256, 384)], [])
-            dma("y", T.tg[1, :], T.tgs[0:64, 1:2], [("tgs", 1, 2)], [])
     for s in SEMAPHORES:
         if count[s]:
             g.wait_ge(T.sem[s], count[s])

@@ -6,10 +6,10 @@ C32 = 402653184.0
 SCRATCH = {"ps": ("psum", [128, 4096], F32)}
 for _t, _l in (
         (BF, "ct 1536 u8 8 ut 1024 wt 512 modb 128 mo2 256 mf2 256 lli 128 one 512 eb 520 w16 512 trs 512 whl 1024 "
-             "tri 128 idn 128 ngt 512 m8 8 cm 72 kb 24 kf 24 kr 64 mk 1152 scn 576 xl 512 x1 512 xk 512 cap 384 jk 385 "
-             "xt 512 e12 12 e0 1 xab 608 mt 512"),
+             "tri 128 idn 128 ngt 512 m8 8 cm 72 kb 24 kf 24 kr 64 mk 1152 scn 576 xl 512 x1 512 xk 512 cap 384 jk 401 "
+             "xt 512 e12 12 e0 1 gt 72 gb 72 xab 608 mt 512"),
         (F32, "uf 8 pj 128 p1 1 k24 24 jb 4 h4 4 l4 4 jd 24 jd1 1 yy 1 p16 1 pr1 1 g64 1 bc 1 hb 1 vl 1 sc 3 sd 3 "
-              "th 384 tt 128 lv 3 lvs 3 n0 1 kh 64 zr 388 ix 1 i32 1 ww 1 ll 1 y1 1 t16 1 nhf 1 hf 1 nvl 1 vhm 1 vlm 1 "
+              "th 384 tt 128 lv 3 lvs 3 n0 1 kh 64 zr 404 ix 1 i32 1 y1 1 t16 1 nhf 1 hf 1 nvl 1 vhm 1 vlm 1 "
               "vhf 1 vlf 1 tab 128 tmp 64 xx 128 pl 1 ph 1 so 1 sg 1 src 24 tgs 2 ysb 384"),
         (U16, "ofl 4 ofr 24 oft 4 ofs 24"),
         (F8, "uq 256 wq 128 kq 1280 xlq 128 x1q 128 xkq 128 xtq 128 xfq 128 abq 152 c0 384 c1 384 c2 384 "
@@ -206,6 +206,7 @@ def rank_program(g, core, T, topo):
     iota("kr", [[1, 64]], 0, 0)
     iota(("ngt", 0, 256), [[0, 256]], -1, 0)
     iota("e0", [[0, 1]], 1, -1)
+    iota("xt", [[0, 512]], 0, 0)
     memset("one", 1.0)
     memset("eb", 0.0)
     memset(("ngt", 256, 512), 0.0)
@@ -215,8 +216,6 @@ def rank_program(g, core, T, topo):
         for b in range(4):
             act(("whl", 512 * h + b, 512 * h + 512, 4), ("one", 0, 128), F.Copy, scale=(x, b, b + 1))
     act(("xl", 3, 512, 4), ("one", 0, 128), F.Copy, scale=0.0)
-    act("xt", "one", F.Copy, scale=0.0)
-    act("xk", "one", F.Copy, scale=0.0)
     quant(*K, ONES, 128, "one", 0)
     ts("tri", "pj", 0.0, A.is_lt)
     ts("yy", "p1", -8.5, A.add, 0.0625, A.mult)
@@ -238,8 +237,10 @@ def rank_program(g, core, T, topo):
     def column(b):
         act(("sc", b, b + 1), ("ps", 512 * b, 512 * b + 1), F.Copy)
 
-    def threshold(b):
+    def spacing(b):
         act(("sd", b, b + 1), ("ps", 512 * b, 512 * b + 1), F.Abs, bias=2.0 ** -120, scale=0.6 * 2.0 ** -23)
+
+    def threshold(b):
         act(("th", 128 * b, 128 * b + 128), "tri", F.Identity, bias=("sc", b, b + 1), scale=("sd", b, b + 1))
 
     for b in range(3):
@@ -256,7 +257,8 @@ def rank_program(g, core, T, topo):
         act(("trs", 3, 512, 4), ("one", 0, 128), F.Copy)
 
     def constants_sent():
-        iota("mo2", [[0, 8], [1, 16], [0, 2]], 1, 0)
+        iota("xk", [[0, 512]], 0, 0)
+        iota("mo2", [[0, 8], [1, 16], [0, 2]], -15, 0)
         iota(("mt", 256, 512), [[0, 256]], 0, 0)
         act("kh", "kr", F.Copy, bias=0.5)
         act(("cap", 64, 384), ("one", 0, 320), F.Copy, scale=1e29)
@@ -265,18 +267,20 @@ def rank_program(g, core, T, topo):
         act(("cm", 0, 64), ("idn", 0, 64), F.Copy)
         act(("cm", 64, 68), ("one", 0, 4), F.Copy, scale=0.0)
         act("jd1", "pr1", F.Copy, bias=-1.0)
-        act(("xt", 259, 260), "e0", F.Relu)
         act("uf", "u8", F.Copy)
         act("jd", "k24", F.Identity, scale=16.0, bias="jd1")
         for e in range(4):
             act(("ut", 512 + e, 1024, 4), ("one", 0, 128), F.Copy, scale=("uf", 4 + e, 5 + e))
         ts(("cm", 68, 72), ("k24", 0, 4), "p16", A.is_equal)
         memset(("zr", 3, 4), -1e29)
+        memset(("zr", 388, 404), 1e29)
         ts("bc", "p1", 447.0, A.add)
         ts("g64", "p1", 65.0, A.is_ge, -1000.0, A.mult)
         ts("hb", "bc", C32, A.add, C32, A.subtract)
         quant(*K, NEG, 128, "ngt", 0)
-        act(("xt", 2, 288, 4), "cm", F.Copy, scale=16.0)
+        act("gb", "cm", F.Copy, scale=40.0, bias=-40.0)
+        act(("xt", 259, 260), "e0", F.Relu)
+        act(("xt", 2, 288, 4), ("one", 0, 72), F.Copy, scale=16.0)
 
     def constants_lists():
         act("vl", "hb", F.Identity, scale=-1.0, bias="bc")
@@ -285,7 +289,7 @@ def rank_program(g, core, T, topo):
         act("kf", "k24", F.Identity, scale=1.0 / 64, bias="g64")
         act("nhf", "hb", F.Copy, scale=-1.0, bias=64.0)
         act("nvl", "vl", F.Copy, scale=-1.0)
-        act("mf2", "mo2", F.Copy, bias=-1.0 / 1024, scale=1.0 / 1024)
+        act("mf2", "mo2", F.Copy, bias=15.0 / 1024, scale=1.0 / 1024)
 
     nd = ("xt", 400, 401)
 
@@ -313,30 +317,34 @@ def rank_program(g, core, T, topo):
             ts(("xl", b, 512, 4), "lli", ("scn", 192 * b + 191, 192 * b + 192), A.is_equal)
 
         column(0)
-        column(1)
+        if t == 0:
+            column(1)
+            spacing(0)
+            spacing(1)
+        else:
+            spacing(0)
+            column(1)
+            spacing(1)
         threshold(0)
         column(2)
+        spacing(2)
         threshold(1)
         threshold(2)
         if t == 0:
             constants_ranks()
-        for b, d in ((0, 1), (1, 0), (0, 2), (1, 2), (0, 0)):
+        for b, d in ((0, 1), (1, 0), (0, 2), (1, 2), (0, 0), (2, 0), (2, 1), (1, 1)):
             against(b, d)
         total(0)
-        against(2, 0)
-        against(2, 1)
-        against(1, 1)
-        total(1)
-        onehot(0)
         against(2, 2)
-        onehot(1)
+        total(1)
         total(2)
-        onehot(2)
+        for b in range(3):
+            onehot(b)
+        ranks = ("scn", 191, 576, 192)
+        ts("lv", ranks, 64.0, A.is_lt)
         quant("xlq", "xls", 0, 128, "xl", 0)
         mm(6, 128, K + (WH,), ("xlq", "xls", 0), True, False)
         mm(6, 128, K + (WL,), ("xlq", "xls", 0), False, True)
-        ranks = ("scn", 191, 576, 192)
-        ts("lv", ranks, 64.0, A.is_lt)
         for b in range(3):
             act(("x1", 384 + 32 * b, 416 + 32 * b, 4), "m8", F.Copy, scale=("lv", b, b + 1))
         ts(("x1", 320, 332, 4), ranks, 64.0, A.is_lt)
@@ -395,28 +403,29 @@ def rank_program(g, core, T, topo):
             for b in range(4):
                 arrived(b)
         scan(("zr", 4, 388), ("ps", 512, 896), "cap", -1e29, A.max, A.min)
-        act("jk", ("zr", 3, 388), F.Sign, bias=("zr", 387, 388), scale=-1.0, acc="ix")
+        act("jk", ("zr", 3, 404), F.Sign, bias=("zr", 387, 388), scale=-1.0, acc="ix")
         ts("e12", ("zr", 35, 388, 32), ("zr", 387, 388), A.is_lt)
+        tt(("tab", 0, 64), ("ps", 0, 64), ("pj", 0, 64), A.add)
         red("i32", "e12", A.add)
+        ts("tmp", ("tab", 0, 64), -7.5 / 1024, A.add)
         if t == 0:
             constants_lists()
-        ts(("xt", 0, 288, 4), "cm", "i32", A.mult, 32.0, A.mult)
-        ts("ww", "i32", 32.0, A.mult, 16.0, A.add)
-        tt(("tab", 0, 64), ("ps", 0, 64), ("pj", 0, 64), A.add)
-        act("tmp", ("tab", 0, 64), F.Copy, bias=-7.5 / 1024)
-        if t == 0:
             arrived(0)
-        tt("ll", "ix", "ww", A.subtract)
-        ts("y1", "ix", -8.5, A.add)
-        ts(("xt", 1, 288, 4), "cm", "ll", A.mult)
-        ts("t16", "y1", 16.0 * C16, A.add, 16.0 * C16, A.subtract)
+        ts("gt", "gb", "i32", A.subtract, 32.0, A.mult)
+        ts(("xt", 0, 288, 4), "cm", "i32", A.mult, 32.0, A.mult)
+        if t == 0:
+            arrived(1)
+        ts(("xt", 1, 288, 4), "gt", "ix", A.add, -16.0, A.max)
+        ts("y1", "ix", 7.5, A.add)
         quant("xtq", "xts", 0, 128, "xt", 0)
         mm(6, 128, K + (TRS,), ("xtq", "xts", 0), True, False)
         mm(6, 128, ("xtq", "xts", 0), K + (NEG,), False, True)
         mm(7, 128, K + (W16,), ("xtq", "xts", 0))
+        ts("t16", "y1", 16.0 * C16, A.add, 16.0 * C16, A.subtract)
+        ts(("tab", 64, 128), "tmp", C16 / 64, A.add, C16 / 64, A.subtract)
         if t == 0:
-            arrived(1)
             arrived(2)
+            arrived(3)
         else:
             quant("wq", "ws", 0, 128, "wt", 0)
         ts(("xab", 96, 608, 2), "mo2", "t16", A.add, "ix", A.is_equal)
@@ -424,8 +433,6 @@ def rank_program(g, core, T, topo):
         ts("oft", ("ps", 3652, 3656), -1.0, A.add)
         quant("xfq", "xfs", 0, 128, "xt", 0)
         mm(6, 128, K + (TRS,), ("xfq", "xfs", 0))
-        if t == 0:
-            arrived(3)
         act("vhm", nd, F.Copy, scale="hb")
         act("vlm", nd, F.Copy, scale="vl")
         pick(rep, reps, 0, 64, c, cs, 384, "oft", 0)
@@ -435,10 +442,9 @@ def rank_program(g, core, T, topo):
             mm(2 + b, 128, K + (EB + 128 * b,), (rep, reps, 0), False, True)
         for b in range(4):
             act(("mt", b, 256, 4), ("ps", 512 * (2 + b), 512 * (2 + b) + 64), F.Copy)
+        ts("xx", "tab", ("ps", 3172, 3173), A.add)
         ts(("xab", 0, 96, 4), "kb", "t16", A.is_equal, "vhm", A.mult)
         ts(("xab", 2, 96, 4), "kb", "t16", A.is_equal, "vlm", A.mult)
-        ts(("tab", 64, 128), "tmp", C16 / 64, A.add, C16 / 64, A.subtract)
-        ts("xx", "tab", ("ps", 3172, 3173), A.add)
         least("ph", ("xx", 64, 128))
         least("pl", ("xx", 0, 64))
         ts(("xab", 1, 96, 4), "kf", "ph", A.is_equal, "vhf", A.mult)
@@ -448,7 +454,7 @@ def rank_program(g, core, T, topo):
         mm(1, 128, ("abq", "abp", 24), ("abq", "abp", 0))
         quant(win, wins, 448, 128, "mt", 0)
         act("so", "pl", F.Copy, scale=-1024.0, bias=-1.0)
-        ts("sg", "ix", -1.0, A.add, "so", A.subtract)
+        ts("sg", "ix", 15.0, A.add, "so", A.subtract)
         if t == 0:
             quant("uq", "us", 128, 128, "ut", 512)
         tt("src", ("ps", 512, 536), "jd", A.max)

@@ -5,23 +5,23 @@ C16 = 12582912.0
 C32 = 402653184.0
 SCRATCH = {"ps": ("psum", [128, 4096], F32)}
 for _t, _l in (
-        (BF, "ct 1536 u8 8 ut 1024 wt 512 modb 128 mo2 256 mf2 256 lli 128 one 512 eb 520 w16 512 trs 512 whl 1024 "
-             "tri 128 idn 128 ngt 512 m8 8 cm 72 kb 24 kf 24 kr 64 mk 1152 scn 576 xl 512 x1 512 xk 512 cap 384 jk 401 "
-             "xt 512 e12 12 e0 1 gt 72 gb 72 xab 608 mt 512"),
-        (F32, "uf 8 pj 128 p1 1 k24 24 jb 4 h4 4 l4 4 jd 24 jd1 1 yy 1 p16 1 pr1 1 g64 1 bc 1 hb 1 vl 1 sc 3 sd 3 "
-              "th 384 tt 128 lv 3 lvs 3 n0 1 kh 64 zr 404 ix 1 i32 1 y1 1 t16 1 nhf 1 hf 1 nvl 1 vhm 1 vlm 1 "
-              "vhf 1 vlf 1 tab 128 tmp 64 xx 128 pl 1 ph 1 so 1 sg 1 src 24 tgs 2 ysb 384"),
+        (BF, "ct 1536 u8 8 ut 1024 wt 512 modb 128 lli 128 one 512 eb 520 w16 512 trs 512 whl 1024 "
+             "tri 128 idn 128 ngt 512 m8 8 cm 72 kb 24 kr 64 mk 1152 scn 576 xl 512 x1 512 xk 512 cap 384 jk 401 "
+             "xt 512 e0 1 gt 72 gb 72 mt 512 nb 512 tl 64 fm 512 bf 512 xm 608 af 512"),
+        (F32, "uf 8 pj 128 p1 1 k24 24 jb 4 h4 4 l4 4 yy 1 p16 1 pr1 1 bc 1 hb 1 vl 1 sc 3 sd 3 "
+              "th 384 tt 128 lv 3 lvs 3 n0 1 kh 64 zr 404 ix 1 i32 1 y1 1 t16 1 tab 64 xx 64 pl 1 qa 1 qb 1 ix16 1 "
+              "tgs 2 ysb 384 yw 512 hn 4 l5 4 nkh 1 rc 1 fl 1 sa 1 sb 1 nd 1 s0 1 a32 1 s2 1 nm 4"),
         (U16, "ofl 4 ofr 24 oft 4 ofs 24"),
-        (F8, "uq 256 wq 128 kq 1280 xlq 128 x1q 128 xkq 128 xtq 128 xfq 128 abq 152 c0 384 c1 384 c2 384 "
-             "win0 576 win1 576 rep0 384 rep1 384 snd0 64 snd1 64"),
-        (U8, "us 256 ws 128 ks 1280 xls 128 x1s 128 xks 128 xts 128 xfs 128 abp 152 cs0 384 cs1 384 cs2 384 "
-             "wins0 576 wins1 576 reps0 384 reps1 384 snds0 64 snds1 64")):
+        (F8, "uq 256 wq 128 kq 1408 xlq 128 x1q 128 xkq 128 xtq 128 fmq 128 afq 128 bfq 128 xmq 152 c0 384 c1 384 "
+             "c2 384 win0 576 win1 576 rep0 384 rep1 384 snd0 64 snd1 64"),
+        (U8, "us 256 ws 128 ks 1408 xls 128 x1s 128 xks 128 xts 128 fms 128 afs 128 bfs 128 xms 152 cs0 384 cs1 384 "
+             "cs2 384 wins0 576 wins1 576 reps0 384 reps1 384 snds0 64 snds1 64")):
     _w = _l.split()
     for _n, _c in zip(_w[::2], _w[1::2]):
         SCRATCH[_n] = ("sbuf", [128, int(_c)], _t)
-NDMA = 26
+NDMA = 24
 SEMAPHORES = ["sv", "ss", "st", "sp", "loc", "arr0", "arr1"] + ["d%d" % i for i in range(NDMA)]
-ONES, W16, TRS, WH, WL, EB, NEG = 0, 128, 256, 384, 512, 640, 1152
+ONES, W16, TRS, WH, WL, EB, NEG, NB = 0, 128, 256, 384, 512, 640, 1152, 1280
 
 
 def rank_program(g, core, T, topo):
@@ -79,6 +79,8 @@ def rank_program(g, core, T, topo):
 
     def view(reg):
         name, lo, hi = reg[0], reg[1], reg[2]
+        if len(reg) > 4:
+            return T[name][reg[4]:reg[5], lo:hi:reg[3]]
         return T[name][:, lo:hi:reg[3]] if len(reg) > 3 else T[name][:, lo:hi]
 
     def run(q, call, rd, wr):
@@ -96,6 +98,16 @@ def rank_program(g, core, T, topo):
 
     def isreg(x):
         return isinstance(x, (str, tuple))
+
+    def rows(x, p0, p1):
+        x = R(x)
+        return (x[0], x[1], x[2], x[3] if len(x) > 3 else 1, p0, p1)
+
+    def top(x):
+        return rows(x, 0, 64)
+
+    def low(x):
+        return rows(x, 64, 128)
 
     def memset(o, v):
         o = R(o)
@@ -157,13 +169,20 @@ def rank_program(g, core, T, topo):
         run("t", lambda: g.tensor.matmul_mx(view(o), view(rl[0]), view(rl[1]), view(rl[2]), view(rl[3]), start, stop),
             rl, [o])
 
-    def pick(o, os, olo, n, win, wins, width, off, off0):
+    def pick_codes(o, olo, n, win, width, off, off0):
         k = (off, off0, off0 + n // 16)
         run("v", lambda: g.vector.tensor_copy(T[o][:, olo:olo + n].bitcast(dt.uint32),
                                               T[win][:, 0:width].bitcast(dt.uint32).indirect(view(k))),
             [(win, 0, width), k], [(o, olo, olo + n)])
-        run("s", lambda: g.scalar.activation(T[os][:, olo:olo + n], T[wins][:, 0:width].indirect(view(k)), F.Copy),
-            [(wins, 0, width), k], [(os, olo, olo + n)])
+
+    def pick_rows(o, olo, n, win, width, off, off0):
+        k = (off, off0, off0 + n // 16)
+        run("s", lambda: g.scalar.activation(T[o][:, olo:olo + n], T[win][:, 0:width].indirect(view(k)), F.Copy),
+            [(win, 0, width), k], [(o, olo, olo + n)])
+
+    def pick(o, os, olo, n, win, wins, width, off, off0):
+        pick_codes(o, olo, n, win, width, off, off0)
+        pick_rows(os, olo, n, wins, width, off, off0)
 
     def iota(o, pattern, base, cm, p0=0, p1=128):
         o = R(o)
@@ -206,25 +225,23 @@ def rank_program(g, core, T, topo):
     iota("kr", [[1, 64]], 0, 0)
     iota(("ngt", 0, 256), [[0, 256]], -1, 0)
     iota("e0", [[0, 1]], 1, -1)
-    iota("xt", [[0, 512]], 0, 0)
     memset("one", 1.0)
-    memset("eb", 0.0)
-    memset(("ngt", 256, 512), 0.0)
     ts("h4", "jb", C32, A.add, C32, A.subtract)
+    ts("yy", "p1", -8.5, A.add, 0.0625, A.mult)
+    memset(("ngt", 256, 512), 0.0)
+    ts("tri", "pj", 0.0, A.is_lt)
     tt("l4", "jb", "h4", A.subtract)
+    ts("p16", "yy", C16, A.add, C16, A.subtract)
     for h, x in ((0, "h4"), (1, "l4")):
         for b in range(4):
             act(("whl", 512 * h + b, 512 * h + 512, 4), ("one", 0, 128), F.Copy, scale=(x, b, b + 1))
     act(("xl", 3, 512, 4), ("one", 0, 128), F.Copy, scale=0.0)
+    act("nb", "one", F.Copy, scale=0.0)
     quant(*K, ONES, 128, "one", 0)
-    ts("tri", "pj", 0.0, A.is_lt)
-    ts("yy", "p1", -8.5, A.add, 0.0625, A.mult)
-    ts("p16", "yy", C16, A.add, C16, A.subtract)
     ts("pr1", "p16", -16.0, A.mult, "p1", A.add)
     ts("idn", "pj", 0.0, A.is_equal)
-    ts(("eb", 4, 516, 4), "pj", 0.0, A.is_equal, 0.5, A.mult)
-    ts(("w16", 0, 512, 4), "modb", "pr1", A.is_equal)
     ts(("trs", 0, 512, 4), "pj", 0.0, A.is_gt)
+    ts(("w16", 0, 512, 4), "modb", "pr1", A.is_equal)
     for e in range(4):
         ts(("ut", e, 512, 4), ("one", 0, 128), ("u8", e, e + 1), A.mult)
     quant("uq", "us", 0, 128, "ut", 0)
@@ -248,6 +265,8 @@ def rank_program(g, core, T, topo):
         scores(0, b)
     quant(*K, WH, 256, "whl", 0)
     ts("m8", ("k24", 0, 8), "p16", A.is_equal, -512.0, A.mult)
+    ts("hn", "h4", -416.0, A.add, 2.0, A.mult)
+    ts("l5", "l4", 2.0, A.mult)
 
     def constants_ranks():
         for i in range(3):
@@ -255,43 +274,49 @@ def rank_program(g, core, T, topo):
         for i in range(2):
             act(("trs", i + 1, 512, 4), ("trs", 0, 512, 4), F.Copy)
         act(("trs", 3, 512, 4), ("one", 0, 128), F.Copy)
+        act(("eb", 0, 512), "one", F.Copy, scale=0.0)
+
+    def constants_gap():
+        ts("rc", "p1", -64.0, A.add)
+        ts("bc", "p1", 447.0, A.add)
+        quant(*K, TRS, 128, "trs", 0)
+
+    def constants_nb():
+        act(("eb", 512, 520), ("one", 0, 8), F.Copy, scale=0.0)
+        for b in range(3):
+            act(("nb", 65 * b, 65 * b + 64, 8), "m8", F.Copy, scale=("hn", b, b + 1))
+            act(("nb", 65 * b + 4, 65 * b + 64, 8), "m8", F.Copy, scale=("l5", b, b + 1))
+            act(("nb", 192 + 33 * b, 224 + 33 * b, 4), "m8", F.Copy)
+
+    def own_side(s):
+        ts(low(("xm", 96 + s, 608, 4)), low("modb"), low("rc"), A.is_equal)
 
     def constants_sent():
         iota("xk", [[0, 512]], 0, 0)
-        iota("mo2", [[0, 8], [1, 16], [0, 2]], -15, 0)
+        iota(("xm", 0, 96, 4), [[128, 3], [0, 8]], 0, 0, 64, 128)
+        iota(("xm", 1, 96, 4), [[0, 3], [16, 8]], 0, 0, 64, 128)
+        iota(("xm", 2, 96, 4), [[0, 24]], 0, 1, 64, 128)
+        iota(("xm", 3, 96, 4), [[0, 24]], 0, 0, 64, 128)
+        iota("fm", [[0, 512]], 0, 0)
         iota(("mt", 256, 512), [[0, 256]], 0, 0)
+        act(("eb", 4, 516, 4), "idn", F.Copy, scale=0.5)
         act("kh", "kr", F.Copy, bias=0.5)
         act(("cap", 64, 384), ("one", 0, 320), F.Copy, scale=1e29)
 
     def constants_travel():
         act(("cm", 0, 64), ("idn", 0, 64), F.Copy)
         act(("cm", 64, 68), ("one", 0, 4), F.Copy, scale=0.0)
-        act("jd1", "pr1", F.Copy, bias=-1.0)
         act("uf", "u8", F.Copy)
-        act("jd", "k24", F.Identity, scale=16.0, bias="jd1")
         for e in range(4):
             act(("ut", 512 + e, 1024, 4), ("one", 0, 128), F.Copy, scale=("uf", 4 + e, 5 + e))
         ts(("cm", 68, 72), ("k24", 0, 4), "p16", A.is_equal)
-        memset(("zr", 3, 4), -1e29)
-        memset(("zr", 388, 404), 1e29)
-        ts("bc", "p1", 447.0, A.add)
-        ts("g64", "p1", 65.0, A.is_ge, -1000.0, A.mult)
-        ts("hb", "bc", C32, A.add, C32, A.subtract)
         quant(*K, NEG, 128, "ngt", 0)
         act("gb", "cm", F.Copy, scale=40.0, bias=-40.0)
         act(("xt", 259, 260), "e0", F.Relu)
         act(("xt", 2, 288, 4), ("one", 0, 72), F.Copy, scale=16.0)
-
-    def constants_lists():
         act("vl", "hb", F.Identity, scale=-1.0, bias="bc")
-        act("hf", "hb", F.Copy, bias=-64.0)
-        act("kb", "k24", F.Identity, scale=16.0, bias="g64")
-        act("kf", "k24", F.Identity, scale=1.0 / 64, bias="g64")
-        act("nhf", "hb", F.Copy, scale=-1.0, bias=64.0)
-        act("nvl", "vl", F.Copy, scale=-1.0)
-        act("mf2", "mo2", F.Copy, bias=15.0 / 1024, scale=1.0 / 1024)
-
-    nd = ("xt", 400, 401)
+        act("kb", "k24", F.Copy, scale=16.0, bias=-16.0)
+        act("nkh", "p1", F.Copy, scale=-1.0, bias=0.5)
 
     for t in range(2):
         c, cs, win, wins = "c%d" % t, "cs%d" % t, "win%d" % t, "wins%d" % t
@@ -332,12 +357,10 @@ def rank_program(g, core, T, topo):
         threshold(2)
         if t == 0:
             constants_ranks()
-        for b, d in ((0, 1), (1, 0), (0, 2), (1, 2), (0, 0), (2, 0), (2, 1), (1, 1)):
+        for b, d in ((0, 1), (1, 0), (0, 2), (1, 2), (0, 0), (2, 0), (2, 1), (1, 1), (2, 2)):
             against(b, d)
-        total(0)
-        against(2, 2)
-        total(1)
-        total(2)
+        for b in range(3):
+            total(b)
         for b in range(3):
             onehot(b)
         ranks = ("scn", 191, 576, 192)
@@ -351,8 +374,16 @@ def rank_program(g, core, T, topo):
         act(("x1", 327, 328), ("lv", 0, 1), F.Copy)
         act(("x1", 331, 332), ("lv", 0, 1), F.Identity, bias=("lv", 1, 2))
         ts(("x1", 0, 256, 4), ("idn", 0, 64), ("lv", 0, 1), A.mult, 512.0, A.mult)
+        act("lvs", "lv", F.Copy, scale=1.0 / 1024)
+        if t == 0:
+            constants_gap()
+            constants_nb()
         run("v", lambda: g.vector.transpose(T.tt[:], T.ps[:, 3072:3200]), [("ps", 3072, 3200)], [whole("tt")])
+        quant("x1q", "x1s", 0, 128, "x1", 0)
         cp("ofl", ("tt", 0, 128, 32))
+        if t == 0:
+            ts("hb", "bc", C32, A.add, C32, A.subtract)
+            ts("tl", ("pj", 0, 64), 0.0, A.is_ge)
         pick(snd, snds, 0, 64, c, cs, 384, "ofl", 0)
         dst = T.cores[rank ^ (1 << t)]
         rid, pid, _ = topo.addr(dst)
@@ -370,29 +401,44 @@ def rank_program(g, core, T, topo):
         clock[(arr, 2 * ne)] = {arr: 2 * ne}
         for o in (win, wins):
             hist.setdefault(o, []).append((384, 448, 1, "-", True, arr, 2 * ne))
-        quant("x1q", "x1s", 0, 128, "x1", 0)
         if t == 0:
             quant(*K, W16, 128, "w16", 0)
+            memset("xt", 0.0)
             constants_sent()
-        act("lvs", "lv", F.Copy, scale=1.0 / 1024)
+        else:
+            quant("wq", "ws", 0, 128, "wt", 0)
         mm(7, 128, K + (ONES,), ("x1q", "x1s", 0))
         mm(0, 128, K + (W16,), ("x1q", "x1s", 0))
         red("n0", ("ps", 3584, 3649), A.min)
-        ts("ofr", ("ps", 96, 120), "n0", A.max)
-        pick(rep, reps, 0, 384, c, cs, 384, "ofr", 0)
         if t == 0:
-            quant(*K, TRS, 128, "trs", 0)
+            own_side(0)
+            own_side(1)
+        ts("ofr", ("ps", 96, 120), "n0", A.max)
+        if t == 0:
+            own_side(2)
+            own_side(3)
+        pick(rep, reps, 0, 384, c, cs, 384, "ofr", 0)
         mm(6, 128, K + (TRS,), ("x1q", "x1s", 0))
         ts(("cap", 0, 64), "kh", "n0", A.subtract, 1e27, A.mult)
         if t == 0:
+            memset(("zr", 3, 4), -1e29)
+            memset(("zr", 388, 404), 1e29)
             constants_travel()
             dma("y", T.wt[:], T.w[:], [], [whole("wt")])
+        else:
+            mm(5, 384, ("wq", "ws", 0), (c, cs, 0))
+            act(("yw", 0, 384), ("ps", 2560, 2944), F.Copy)
         mm(1, 384, (win, wins, 384), (rep, reps, 0))
         for b in range(3):
             ts(("xk", b, 256, 4), "kr", ("ps", 3152 + b, 3153 + b), A.is_equal, ("lvs", b, b + 1), A.mult)
         quant("xkq", "xks", 0, 128, "xk", 0)
-        mm(0, 128, K + (WH,), ("xkq", "xks", 0), True, False)
-        mm(0, 128, K + (WL,), ("xkq", "xks", 0), False, True)
+        if t == 0:
+            quant(*K, NB, 128, "nb", 0)
+            quant("uq", "us", 128, 128, "ut", 512)
+        mm(7, 128, ("xkq", "xks", 0), K + (W16,))
+        mm(0, 128, ("xkq", "xks", 0), K + (NB,))
+        mm(6, 128, K + (WH,), ("xkq", "xks", 0), True, False)
+        mm(6, 128, K + (WL,), ("xkq", "xks", 0), False, True)
 
         def arrived(b):
             if t == 0:
@@ -402,82 +448,106 @@ def rank_program(g, core, T, topo):
         if t == 1:
             for b in range(4):
                 arrived(b)
+
+        def left_side(e):
+            act(("af", e, 512, 4), ("ps", 3584, 3712), F.Copy, scale=1024.0)
+
         scan(("zr", 4, 388), ("ps", 512, 896), "cap", -1e29, A.max, A.min)
+        left_side(0)
+        left_side(1)
         act("jk", ("zr", 3, 404), F.Sign, bias=("zr", 387, 388), scale=-1.0, acc="ix")
-        ts("e12", ("zr", 35, 388, 32), ("zr", 387, 388), A.is_lt)
-        tt(("tab", 0, 64), ("ps", 0, 64), ("pj", 0, 64), A.add)
-        red("i32", "e12", A.add)
-        ts("tmp", ("tab", 0, 64), -7.5 / 1024, A.add)
         if t == 0:
-            constants_lists()
             arrived(0)
-        ts("gt", "gb", "i32", A.subtract, 32.0, A.mult)
-        ts(("xt", 0, 288, 4), "cm", "i32", A.mult, 32.0, A.mult)
+        runs = ("mk", 0, 12)
+        ts(runs, ("zr", 35, 388, 32), ("zr", 387, 388), A.is_lt)
         if t == 0:
             arrived(1)
+        red("i32", runs, A.add)
+        if t == 0:
+            arrived(2)
+        ts("gt", "gb", "i32", A.subtract, 32.0, A.mult)
+        ts(("xt", 0, 288, 4), "cm", "i32", A.mult, 32.0, A.mult)
+        tt("tab", ("ps", 3072, 3136), "kr", A.add)
+        if t == 0:
+            act("bf", "one", F.Copy, scale=0.0)
+        left_side(2)
+        left_side(3)
+        act("s0", "i32", F.Identity, scale=-32.0, bias="hb")
+        act("a32", "i32", F.Copy, scale=32.0)
+        act("s2", "ix", F.Identity, scale=-1.0, bias="a32")
+        act("ix16", "ix", F.Copy, bias=16.0)
         ts(("xt", 1, 288, 4), "gt", "ix", A.add, -16.0, A.max)
         ts("y1", "ix", 7.5, A.add)
         quant("xtq", "xts", 0, 128, "xt", 0)
         mm(6, 128, K + (TRS,), ("xtq", "xts", 0), True, False)
         mm(6, 128, ("xtq", "xts", 0), K + (NEG,), False, True)
-        mm(7, 128, K + (W16,), ("xtq", "xts", 0))
-        ts("t16", "y1", 16.0 * C16, A.add, 16.0 * C16, A.subtract)
-        ts(("tab", 64, 128), "tmp", C16 / 64, A.add, C16 / 64, A.subtract)
+        mm(1, 128, K + (W16,), ("xtq", "xts", 0))
+        ts("t16", "y1", 16.0 * C16, A.add, 16.0 * C16 + 16.0, A.subtract)
         if t == 0:
-            arrived(2)
             arrived(3)
         else:
-            quant("wq", "ws", 0, 128, "wt", 0)
-        ts(("xab", 96, 608, 2), "mo2", "t16", A.add, "ix", A.is_equal)
-        least(nd, ("ps", 3072, 3137))
-        ts("oft", ("ps", 3652, 3656), -1.0, A.add)
-        quant("xfq", "xfs", 0, 128, "xt", 0)
-        mm(6, 128, K + (TRS,), ("xfq", "xfs", 0))
-        act("vhm", nd, F.Copy, scale="hb")
-        act("vlm", nd, F.Copy, scale="vl")
+            quant("afq", "afs", 0, 128, "af", 0)
+        for e in range(4):
+            ts(top(("xm", 96 + e, 608, 4)), top("modb"), top("t16"), A.add, top("ix"), A.is_equal)
+        least("nd", ("ps", 3072, 3137))
+        ts("oft", ("ps", 580, 584), -1.0, A.add)
+        ts(("fm", 0, 256, 4), "tl", "nd", A.is_gt)
+        quant("fmq", "fms", 0, 128, "fm", 0)
+        for b in (6, 7):
+            mm(b, 128, K + (ONES,), ("fmq", "fms", 0))
+        for e, x in ((0, "s0"), (1, "vl"), (2, "s2"), (3, -15.0)):
+            act(("nm", e, e + 1), "nd", F.Copy, scale=x)
         pick(rep, reps, 0, 64, c, cs, 384, "oft", 0)
-        act("vhf", nd, F.Identity, scale="nhf", bias="hf")
-        act("vlf", nd, F.Identity, scale="nvl", bias="vl")
+        for e in range(4):
+            ts(top(("xm", e, 96, 4)), top("kb"), top("t16"), A.is_equal, top(("nm", e, e + 1)), A.mult)
         for b in range(4):
             mm(2 + b, 128, K + (EB + 128 * b,), (rep, reps, 0), False, True)
+        act(("jk", 0, 32), ("ps", 3072, 3104), F.Sign, bias="nkh", acc="sa")
+        act(("jk", 32, 64), ("ps", 3104, 3136), F.Sign, bias="nkh", acc="sb")
+        if t == 0:
+            quant("afq", "afs", 0, 128, "af", 0)
+        ts("fl", ("ps", 3647, 3648), "p1", A.is_ge)
+        mm(7, 128, ("fmq", "fms", 0), K + (ONES,))
         for b in range(4):
             act(("mt", b, 256, 4), ("ps", 512 * (2 + b), 512 * (2 + b) + 64), F.Copy)
-        ts("xx", "tab", ("ps", 3172, 3173), A.add)
-        ts(("xab", 0, 96, 4), "kb", "t16", A.is_equal, "vhm", A.mult)
-        ts(("xab", 2, 96, 4), "kb", "t16", A.is_equal, "vlm", A.mult)
-        least("ph", ("xx", 64, 128))
-        least("pl", ("xx", 0, 64))
-        ts(("xab", 1, 96, 4), "kf", "ph", A.is_equal, "vhf", A.mult)
-        ts(("xab", 3, 96, 4), "kf", "ph", A.is_equal, "vlf", A.mult)
-        ts(("xab", 97, 608, 2), "mf2", "ph", A.add, "pl", A.is_equal)
-        quant("abq", "abp", 0, 152, "xab", 0)
-        mm(1, 128, ("abq", "abp", 24), ("abq", "abp", 0))
+        act("qa", "nd", F.Copy, scale="ix16", bias=-1.0)
+        act("qb", "nd", F.Copy, scale=1024.0, bias=-1024.0)
+        quant("xmq", "xms", 0, 152, "xm", 0)
+        mm(1, 128, ("xmq", "xms", 24), ("xmq", "xms", 0), True, False)
+        run("v", lambda: g.vector.tensor_scalar(T.bf[:, 0:96:2], T.ps[:, 0:48], T.fl[:], None, A.mult),
+            [("ps", 0, 48), whole("fl")], [("bf", 0, 96, 4), ("bf", 2, 96, 4)])
+        ts(("bf", 1, 96, 4), ("ps", 48, 72), "sa", A.mult, "fl", A.mult)
+        ts(("bf", 3, 96, 4), ("ps", 48, 72), "sb", A.mult, "fl", A.mult)
+        quant("bfq", "bfs", 0, 128, "bf", 0)
+        mm(1, 128, ("afq", "afs", 0), ("bfq", "bfs", 0), False, True)
+        ts("xx", "tab", ("ps", 3584, 3585), A.subtract, 1.0, A.add)
         quant(win, wins, 448, 128, "mt", 0)
-        act("so", "pl", F.Copy, scale=-1024.0, bias=-1.0)
-        ts("sg", "ix", 15.0, A.add, "so", A.subtract)
+        least("pl", "xx")
+        cp("ofs", ("ps", 512, 536))
+        ts(("tgs", t, t + 1), "pl", "qb", A.mult, "qa", A.add)
         if t == 0:
-            quant("uq", "us", 128, 128, "ut", 512)
-        tt("src", ("ps", 512, 536), "jd", A.max)
-        cp("ofs", "src")
-        ts(("tgs", t, t + 1), nd, "sg", A.mult, "so", A.add)
-        for b in range(3):
-            pick(nc, ncs, 128 * b, 128, win, wins, 512, "ofs", 8 * b)
-            if t == 0:
+            dma("y", T.tg[0, :], T.tgs[0:64, 0:1], [("tgs", 0, 1)], [])
+            for b in range(3):
+                pick(nc, ncs, 128 * b, 128, win, wins, 512, "ofs", 8 * b)
                 scores(1, b)
-            else:
-                mm((6, 7, 0)[b], 128, ("wq", "ws", 0), (nc, ncs, 128 * b))
-                dma("y", T.oc[:, 512 * b:512 * b + 512], T[nc][:, 128 * b:128 * b + 128].bitcast(dt.uint8),
-                    [(nc, 128 * b, 128 * b + 128)], [])
-            if b == 0:
-                dma("y", T.tg[t, :], T.tgs[0:64, t:t + 1], [("tgs", t, t + 1)], [])
-        if t == 1:
+        else:
+            mm(2, 128, ("wq", "ws", 0), (win, wins, 384))
+            act(("yw", 384, 512), ("ps", 1024, 1152), F.Copy)
+            pick_rows(ncs, 0, 192, wins, 512, "ofs", 0)
+            pick_rows("ysb", 192, 192, "yw", 512, "ofs", 12)
+            pick_rows(ncs, 192, 192, wins, 512, "ofs", 12)
+            for b in range(2):
+                pick_codes(nc, 192 * b, 192, win, 512, "ofs", 12 * b)
+                dma("y", T.oc[:, 768 * b:768 * b + 768], T[nc][:, 192 * b:192 * b + 192].bitcast(dt.uint8),
+                    [(nc, 192 * b, 192 * b + 192)], [])
+                if b == 0:
+                    dma("y", T.tg[1, :], T.tgs[0:64, 1:2], [("tgs", 1, 2)], [])
+                    dma("y", T.y[:, 192:384], T.ysb[:, 192:384], [("ysb", 192, 384)], [])
+            run("v", lambda: g.vector.tensor_copy(T.ysb[:, 0:192], T.yw[:].indirect(T.ofs[:, 0:12])),
+                [whole("yw"), ("ofs", 0, 12)], [("ysb", 0, 192)])
             for k in range(4):
-                dma("ys"[k // 2], T.osc[4 * k:4 * k + 4, :], T[ncs][32 * k:32 * k + 4, 0:384], [whole(ncs)], [])
-            cp(("ysb", 0, 128), ("ps", 3072, 3200))
-            cp(("ysb", 128, 256), ("ps", 3584, 3712))
-            act(("ysb", 256, 384), ("ps", 0, 128), F.Copy)
-            dma("y", T.y[:, 0:256], T.ysb[:, 0:256], [("ysb", 0, 256)], [])
-            dma("s", T.y[:, 256:384], T.ysb[:, 256:384], [("ysb", 256, 384)], [])
+                dma("s", T.osc[4 * k:4 * k + 4, :], T[ncs][32 * k:32 * k + 4, 0:384], [whole(ncs)], [])
+            dma("y", T.y[:, 0:192], T.ysb[:, 0:192], [("ysb", 0, 192)], [])
     for s in SEMAPHORES:
         if count[s]:
             g.wait_ge(T.sem[s], count[s])

from concourse.mybir import dt, AluOpType as A, AxisListType, ActivationFunctionType as F

F8, U8, BF, F32, U16 = "float8_e4m3fn_x4", "uint8", "bfloat16", "float32", "uint16"
C16 = 12582912.0
C32 = 402653184.0
SCRATCH = {"ps": ("psum", [128, 4096], F32)}
for _t, _l in (
        (BF, "ct 1536 u8 8 ut 1024 wt 512 modb 128 lli 128 one 512 eb 520 w16 512 trs 512 whl 1024 "
             "tri 128 idn 128 ngt 512 m8 8 cm 72 kb 24 kr 64 mk 1152 scn 576 xl 512 x1 512 xk 512 cap 384 jk 401 "
             "xt 512 e0 1 gt 72 gb 72 mt 512 nb 512 tl 64 fm 512 bf 512 xm 608 af 512"),
        (F32, "uf 8 pj 128 p1 1 k24 24 jb 4 h4 4 l4 4 yy 1 p16 1 pr1 1 bc 1 hb 1 vl 1 sc 3 sd 3 "
              "th 384 tt 128 lv 3 lvs 3 n0 1 kh 64 zr 404 ix 1 i32 1 y1 1 t16 1 tab 64 xx 64 pl 1 qa 1 qb 1 ix16 1 "
              "tgs 2 ysb 384 yw 512 hn 4 l5 4 nkh 1 rc 1 fl 1 sa 1 sb 1 nd 1 s0 1 a32 1 s2 1 nm 4"),
        (U16, "ofl 4 ofr 24 oft 4 ofs 24"),
        (F8, "uq 256 wq 128 kq 1408 xlq 128 x1q 128 xkq 128 xtq 128 fmq 128 afq 128 bfq 128 xmq 152 c0 384 c1 384 "
             "c2 384 win0 576 win1 576 rep0 384 rep1 384 snd0 64 snd1 64"),
        (U8, "us 256 ws 128 ks 1408 xls 128 x1s 128 xks 128 xts 128 fms 128 afs 128 bfs 128 xms 152 cs0 384 cs1 384 "
             "cs2 384 wins0 576 wins1 576 reps0 384 reps1 384 snds0 64 snds1 64")):
    _w = _l.split()
    for _n, _c in zip(_w[::2], _w[1::2]):
        SCRATCH[_n] = ("sbuf", [128, int(_c)], _t)
NDMA = 24
SEMAPHORES = ["sv", "ss", "st", "sp", "loc", "arr0", "arr1"] + ["d%d" % i for i in range(NDMA)]
ONES, W16, TRS, WH, WL, EB, NEG, NB = 0, 128, 256, 384, 512, 640, 1152, 1280


def rank_program(g, core, T, topo):
    rank = T.rank_of(core)
    if rank is None:
        return
    queue = {"v": g.vector, "s": g.scalar, "t": g.tensor, "p": g, "y": g.sync}
    own = {"v": "sv", "s": "ss", "t": "st", "p": "sp"}
    count = {s: 0 for s in SEMAPHORES}
    clock = {}
    known = {q: {} for q in queue}
    hist = {}
    ndma = [0]
    part = [False]

    def merge(a, b):
        for s, v in b.items():
            if a.get(s, 0) < v:
                a[s] = v

    def dep(q, rd, wr):
        need = {}
        for lst, w in ((rd, False), (wr, True)):
            for reg in lst:
                name, lo, hi = reg[0], reg[1], reg[2]
                st = reg[3] if len(reg) > 3 else 1
                psum = name == "ps"
                if psum:
                    lo, hi, st = lo // 512 * 512, (hi + 511) // 512 * 512, 1
                for (l2, h2, s2, q2, w2, sem, val) in hist.get(name, ()):
                    if l2 >= hi or lo >= h2 or (st == s2 and st > 1 and (lo - l2) % st):
                        continue
                    if psum and q == q2 and (q == "t" or not (w or w2)):
                        continue
                    if w or w2 or (psum and q != q2):
                        need[sem] = max(need.get(sem, 0), val)
        for sem in sorted(need, key=lambda s: s == own.get(q)):
            if known[q].get(sem, 0) < need[sem]:
                queue[q].wait_ge(T.sem[sem], need[sem])
                merge(known[q], clock[(sem, need[sem])])

    def note(q, rd, wr, sem, val):
        c = dict(known[q])
        c[sem] = val
        if (sem, val - 1) in clock:
            merge(c, clock[(sem, val - 1)])
        clock[(sem, val)] = c
        for lst, w in ((rd, False), (wr, True)):
            for reg in lst:
                name, lo, hi = reg[0], reg[1], reg[2]
                st = reg[3] if len(reg) > 3 else 1
                if name == "ps":
                    lo, hi, st = lo // 512 * 512, (hi + 511) // 512 * 512, 1
                hist.setdefault(name, []).append((lo, hi, st, q, w, sem, val))

    def view(reg):
        name, lo, hi = reg[0], reg[1], reg[2]
        if len(reg) > 4:
            return T[name][reg[4]:reg[5], lo:hi:reg[3]]
        return T[name][:, lo:hi:reg[3]] if len(reg) > 3 else T[name][:, lo:hi]

    def run(q, call, rd, wr):
        dep(q, rd, wr)
        sem = own[q]
        count[sem] += 1
        call().then_inc(T.sem[sem], 1)
        note(q, rd, wr, sem, count[sem])

    def whole(name):
        return (name, 0, SCRATCH[name][1][1])

    def R(x):
        return whole(x) if isinstance(x, str) else x

    def isreg(x):
        return isinstance(x, (str, tuple))

    def rows(x, p0, p1):
        x = R(x)
        return (x[0], x[1], x[2], x[3] if len(x) > 3 else 1, p0, p1)

    def top(x):
        return rows(x, 0, 64)

    def low(x):
        return rows(x, 64, 128)

    def memset(o, v):
        o = R(o)
        run("v", lambda: g.vector.memset(view(o), v), [], [o])

    def ts(o, i, s1, op0, s2=None, op1=None):
        o, i = R(o), R(i)
        rd = [i] + [R(s) for s in (s1, s2) if isreg(s)]
        a = view(R(s1)) if isreg(s1) else s1
        b = view(R(s2)) if isreg(s2) else s2
        if op1 is None:
            run("v", lambda: g.vector.tensor_scalar(view(o), view(i), a, None, op0), rd, [o])
        else:
            run("v", lambda: g.vector.tensor_scalar(view(o), view(i), a, b, op0, op1), rd, [o])

    def tt(o, a, b, op):
        o, a, b = R(o), R(a), R(b)
        run("v", lambda: g.vector.tensor_tensor(view(o), view(a), view(b), op), [a, b], [o])

    def cp(o, i):
        o, i = R(o), R(i)
        run("v", lambda: g.vector.tensor_copy(view(o), view(i)), [i], [o])

    def red(o, i, op):
        o, i = R(o), R(i)
        run("v", lambda: g.vector.tensor_reduce(view(o), view(i), AxisListType.X, op), [i], [o])

    def least(o, i):
        o, i = R(o), R(i)
        run("v", lambda: g.vector.tensor_reduce(view(o), view(i), AxisListType.X, A.min, apply_absolute_value=True),
            [i], [o])

    def scan(o, a, b, init, op0, op1):
        o, a, b = R(o), R(a), R(b)
        run("v", lambda: g.vector.tensor_tensor_scan(view(o), view(a), view(b), init, op0, op1), [a, b], [o])

    def act(o, i, func, bias=None, scale=None, acc=None):
        o, i = R(o), R(i)
        rd, wr, kw = [i], [o], {}
        for k, x in (("bias", bias), ("scale", scale)):
            if isreg(x):
                rd.append(R(x))
                kw[k] = view(R(x))
            elif x is not None:
                kw[k] = x
        if acc is not None:
            wr.append(R(acc))
            kw["accum_out"] = view(R(acc))
        run("s", lambda: g.scalar.activation(view(o), view(i), func, **kw), rd, wr)

    def quant(qn, sn, lo, n, src, slo):
        s = (src, slo, slo + 4 * n)
        run("v", lambda: g.vector.quantize_mx(T[qn][:, lo:lo + n], T[sn][:, lo:lo + n], view(s)),
            [s], [(qn, lo, lo + n), (sn, lo, lo + n)])

    def mm(bank, n, l, r, start=True, stop=True):
        o = ("ps", 512 * bank, 512 * bank + n)
        rl = [(l[0], l[2], l[2] + 128), (l[1], l[2], l[2] + 128), (r[0], r[2], r[2] + n), (r[1], r[2], r[2] + n)]
        run("t", lambda: g.tensor.matmul_mx(view(o), view(rl[0]), view(rl[1]), view(rl[2]), view(rl[3]), start, stop),
            rl, [o])

    def pick_codes(o, olo, n, win, width, off, off0):
        k = (off, off0, off0 + n // 16)
        run("v", lambda: g.vector.tensor_copy(T[o][:, olo:olo + n].bitcast(dt.uint32),
                                              T[win][:, 0:width].bitcast(dt.uint32).indirect(view(k))),
            [(win, 0, width), k], [(o, olo, olo + n)])

    def pick_rows(o, olo, n, win, width, off, off0):
        k = (off, off0, off0 + n // 16)
        run("s", lambda: g.scalar.activation(T[o][:, olo:olo + n], T[win][:, 0:width].indirect(view(k)), F.Copy),
            [(win, 0, width), k], [(o, olo, olo + n)])

    def pick(o, os, olo, n, win, wins, width, off, off0):
        pick_codes(o, olo, n, win, width, off, off0)
        pick_rows(os, olo, n, wins, width, off, off0)

    def iota(o, pattern, base, cm, p0=0, p1=128):
        o = R(o)
        st = o[3] if len(o) > 3 else 1
        if part[0] or p1 - p0 < 128:
            g.wait_ge(T.sem["sp"], count["sp"])
            merge(known["p"], clock[("sp", count["sp"])])
        part[0] = p1 - p0 < 128
        run("p", lambda: g.iota(T[o[0]][p0:p1, o[1]:o[2]:st], pattern, base, cm, allow_small_or_imprecise_dtypes=True),
            [], [o])

    def dma(q, out, in_, rd, wr):
        dep(q, rd, wr)
        sem = "d%d" % ndma[0]
        ndma[0] += 1
        count[sem] = 16
        queue[q].dma_start(out, in_).then_inc(T.sem[sem], 16)
        note(q, rd, wr, sem, 16)

    K = ("kq", "ks")

    dma("y", T.u8[:], T.u[:, 0:8], [], [whole("u8")])
    dma("s", T.ct[:, 0:512], T.c[:, 0:512], [], [("ct", 0, 512)])
    dma("y", T.ct[:, 512:1024], T.c[:, 512:1024], [], [("ct", 512, 1024)])
    dma("s", T.ct[:, 1024:1536], T.c[:, 1024:1536], [], [("ct", 1024, 1536)])

    iota("jb", [[128, 4]], 0, 1)
    iota("p1", [[0, 1]], 1, 1)
    iota("pj", [[1, 128]], 0, -1)
    iota("lli", [[16, 4], [0, 2], [1, 16]], 0, 0)
    iota("modb", [[0, 8], [1, 16]], 1, 0)
    iota("k24", [[1, 24]], 0, 0)
    iota("x1", [[0, 512]], 0, 0)
    iota(("x1", 1, 320, 4), [[16, 5], [0, 16]], 0, 0, 0, 1)
    iota(("x1", 2, 320, 4), [[0, 5], [1, 16]], 0, 0, 0, 1)
    iota(("x1", 385, 480, 4), [[0, 24]], 0, 1, 0, 16)
    iota(("x1", 385, 448, 4), [[16, 16]], 0, 0, 32, 48)
    iota(("x1", 449, 480, 4), [[0, 8]], 240, 0, 32, 48)
    iota(("x1", 449, 480, 4), [[16, 8]], 16, 0, 64, 80)
    iota("kr", [[1, 64]], 0, 0)
    iota(("ngt", 0, 256), [[0, 256]], -1, 0)
    iota("e0", [[0, 1]], 1, -1)
    memset("one", 1.0)
    ts("h4", "jb", C32, A.add, C32, A.subtract)
    ts("yy", "p1", -8.5, A.add, 0.0625, A.mult)
    memset(("ngt", 256, 512), 0.0)
    ts("tri", "pj", 0.0, A.is_lt)
    tt("l4", "jb", "h4", A.subtract)
    ts("p16", "yy", C16, A.add, C16, A.subtract)
    for h, x in ((0, "h4"), (1, "l4")):
        for b in range(4):
            act(("whl", 512 * h + b, 512 * h + 512, 4), ("one", 0, 128), F.Copy, scale=(x, b, b + 1))
    act(("xl", 3, 512, 4), ("one", 0, 128), F.Copy, scale=0.0)
    act("nb", "one", F.Copy, scale=0.0)
    quant(*K, ONES, 128, "one", 0)
    ts("pr1", "p16", -16.0, A.mult, "p1", A.add)
    ts("idn", "pj", 0.0, A.is_equal)
    ts(("trs", 0, 512, 4), "pj", 0.0, A.is_gt)
    ts(("w16", 0, 512, 4), "modb", "pr1", A.is_equal)
    for e in range(4):
        ts(("ut", e, 512, 4), ("one", 0, 128), ("u8", e, e + 1), A.mult)
    quant("uq", "us", 0, 128, "ut", 0)

    def scores(t, b):
        c, s, u = "c%d" % t, "cs%d" % t, ("uq", "us", 128 * t)
        mm(b, 128, (c, s, 128 * b), u)
        mm(3 + b, 128, u, (c, s, 128 * b))

    def column(b):
        act(("sc", b, b + 1), ("ps", 512 * b, 512 * b + 1), F.Copy)

    def spacing(b):
        act(("sd", b, b + 1), ("ps", 512 * b, 512 * b + 1), F.Abs, bias=2.0 ** -120, scale=0.6 * 2.0 ** -23)

    def threshold(b):
        act(("th", 128 * b, 128 * b + 128), "tri", F.Identity, bias=("sc", b, b + 1), scale=("sd", b, b + 1))

    for b in range(3):
        quant("c0", "cs0", 128 * b, 128, "ct", 512 * b)
        scores(0, b)
    quant(*K, WH, 256, "whl", 0)
    ts("m8", ("k24", 0, 8), "p16", A.is_equal, -512.0, A.mult)
    ts("hn", "h4", -416.0, A.add, 2.0, A.mult)
    ts("l5", "l4", 2.0, A.mult)

    def constants_ranks():
        for i in range(3):
            act(("w16", i + 1, 512, 4), ("w16", 0, 512, 4), F.Copy)
        for i in range(2):
            act(("trs", i + 1, 512, 4), ("trs", 0, 512, 4), F.Copy)
        act(("trs", 3, 512, 4), ("one", 0, 128), F.Copy)
        act(("eb", 0, 512), "one", F.Copy, scale=0.0)

    def constants_gap():
        ts("rc", "p1", -64.0, A.add)
        ts("bc", "p1", 447.0, A.add)
        quant(*K, TRS, 128, "trs", 0)

    def constants_nb():
        act(("eb", 512, 520), ("one", 0, 8), F.Copy, scale=0.0)
        for b in range(3):
            act(("nb", 65 * b, 65 * b + 64, 8), "m8", F.Copy, scale=("hn", b, b + 1))
            act(("nb", 65 * b + 4, 65 * b + 64, 8), "m8", F.Copy, scale=("l5", b, b + 1))
            act(("nb", 192 + 33 * b, 224 + 33 * b, 4), "m8", F.Copy)

    def own_side(s):
        ts(low(("xm", 96 + s, 608, 4)), low("modb"), low("rc"), A.is_equal)

    def constants_sent():
        iota("xk", [[0, 512]], 0, 0)
        iota(("xm", 0, 96, 4), [[128, 3], [0, 8]], 0, 0, 64, 128)
        iota(("xm", 1, 96, 4), [[0, 3], [16, 8]], 0, 0, 64, 128)
        iota(("xm", 2, 96, 4), [[0, 24]], 0, 1, 64, 128)
        iota(("xm", 3, 96, 4), [[0, 24]], 0, 0, 64, 128)
        iota("fm", [[0, 512]], 0, 0)
        iota(("mt", 256, 512), [[0, 256]], 0, 0)
        act(("eb", 4, 516, 4), "idn", F.Copy, scale=0.5)
        act("kh", "kr", F.Copy, bias=0.5)
        act(("cap", 64, 384), ("one", 0, 320), F.Copy, scale=1e29)

    def constants_travel():
        act(("cm", 0, 64), ("idn", 0, 64), F.Copy)
        act(("cm", 64, 68), ("one", 0, 4), F.Copy, scale=0.0)
        act("uf", "u8", F.Copy)
        for e in range(4):
            act(("ut", 512 + e, 1024, 4), ("one", 0, 128), F.Copy, scale=("uf", 4 + e, 5 + e))
        ts(("cm", 68, 72), ("k24", 0, 4), "p16", A.is_equal)
        quant(*K, NEG, 128, "ngt", 0)
        act("gb", "cm", F.Copy, scale=40.0, bias=-40.0)
        act(("xt", 259, 260), "e0", F.Relu)
        act(("xt", 2, 288, 4), ("one", 0, 72), F.Copy, scale=16.0)
        act("vl", "hb", F.Identity, scale=-1.0, bias="bc")
        act("kb", "k24", F.Copy, scale=16.0, bias=-16.0)
        act("nkh", "p1", F.Copy, scale=-1.0, bias=0.5)

    for t in range(2):
        c, cs, win, wins = "c%d" % t, "cs%d" % t, "win%d" % t, "wins%d" % t
        rep, reps, snd, snds = "rep%d" % t, "reps%d" % t, "snd%d" % t, "snds%d" % t
        nc, ncs = "c%d" % (t + 1), "cs%d" % (t + 1)
        dma("y", T[win][:, 0:384].bitcast(dt.uint8), T[c][:, 0:384].bitcast(dt.uint8), [whole(c)], [(win, 0, 384)])
        dma("y", T[wins][:, 0:384], T[cs][:, 0:384], [whole(cs)], [(wins, 0, 384)])
        dma("y", T[win][:, 448:512].bitcast(dt.uint8), T[c][:, 0:64].bitcast(dt.uint8), [(c, 0, 64)], [(win, 448, 512)])
        dma("y", T[wins][:, 448:512], T[cs][:, 0:64], [(cs, 0, 64)], [(wins, 448, 512)])

        def against(b, d):
            o, i = ("mk", 384 * b + 128 * d, 384 * b + 128 * d + 128), ("ps", 512 * (3 + d), 512 * (3 + d) + 128)
            if b == d:
                tt(o, i, ("th", 128 * b, 128 * b + 128), A.is_lt)
            else:
                ts(o, i, ("sc", b, b + 1), A.is_le if d < b else A.is_lt)

        def total(b):
            scan(("scn", 192 * b, 192 * b + 192), ("mk", 384 * b, 384 * b + 192), ("mk", 384 * b + 192, 384 * b + 384),
                 0.0, A.add, A.add)

        def onehot(b):
            ts(("xl", b, 512, 4), "lli", ("scn", 192 * b + 191, 192 * b + 192), A.is_equal)

        column(0)
        if t == 0:
            column(1)
            spacing(0)
            spacing(1)
        else:
            spacing(0)
            column(1)
            spacing(1)
        threshold(0)
        column(2)
        spacing(2)
        threshold(1)
        threshold(2)
        if t == 0:
            constants_ranks()
        for b, d in ((0, 1), (1, 0), (0, 2), (1, 2), (0, 0), (2, 0), (2, 1), (1, 1), (2, 2)):
            against(b, d)
        for b in range(3):
            total(b)
        for b in range(3):
            onehot(b)
        ranks = ("scn", 191, 576, 192)
        ts("lv", ranks, 64.0, A.is_lt)
        quant("xlq", "xls", 0, 128, "xl", 0)
        mm(6, 128, K + (WH,), ("xlq", "xls", 0), True, False)
        mm(6, 128, K + (WL,), ("xlq", "xls", 0), False, True)
        for b in range(3):
            act(("x1", 384 + 32 * b, 416 + 32 * b, 4), "m8", F.Copy, scale=("lv", b, b + 1))
        ts(("x1", 320, 332, 4), ranks, 64.0, A.is_lt)
        act(("x1", 327, 328), ("lv", 0, 1), F.Copy)
        act(("x1", 331, 332), ("lv", 0, 1), F.Identity, bias=("lv", 1, 2))
        ts(("x1", 0, 256, 4), ("idn", 0, 64), ("lv", 0, 1), A.mult, 512.0, A.mult)
        act("lvs", "lv", F.Copy, scale=1.0 / 1024)
        if t == 0:
            constants_gap()
            constants_nb()
        run("v", lambda: g.vector.transpose(T.tt[:], T.ps[:, 3072:3200]), [("ps", 3072, 3200)], [whole("tt")])
        quant("x1q", "x1s", 0, 128, "x1", 0)
        cp("ofl", ("tt", 0, 128, 32))
        if t == 0:
            ts("hb", "bc", C32, A.add, C32, A.subtract)
            ts("tl", ("pj", 0, 64), 0.0, A.is_ge)
        pick(snd, snds, 0, 64, c, cs, 384, "ofl", 0)
        dst = T.cores[rank ^ (1 << t)]
        rid, pid, _ = topo.addr(dst)
        m = topo.mask(core, dst)
        ne = len(topo.engines(core, dst))
        arr = "arr%d" % t
        for o, s in ((win, snd), (wins, snds)):
            dep("p", [whole(s)], [])
            w, i = T[o][:, 384:448], T[s][:, 0:64]
            if o == win:
                w, i = w.bitcast(dt.uint8), i.bitcast(dt.uint8)
            g.remote_dma(w, i, T.sem[arr], T.sem["loc"], pid, rid, m)
            count["loc"] += ne
        count[arr] = 2 * ne
        clock[(arr, 2 * ne)] = {arr: 2 * ne}
        for o in (win, wins):
            hist.setdefault(o, []).append((384, 448, 1, "-", True, arr, 2 * ne))
        if t == 0:
            quant(*K, W16, 128, "w16", 0)
            memset("xt", 0.0)
            constants_sent()
        else:
            quant("wq", "ws", 0, 128, "wt", 0)
        mm(7, 128, K + (ONES,), ("x1q", "x1s", 0))
        mm(0, 128, K + (W16,), ("x1q", "x1s", 0))
        red("n0", ("ps", 3584, 3649), A.min)
        if t == 0:
            own_side(0)
            own_side(1)
        ts("ofr", ("ps", 96, 120), "n0", A.max)
        if t == 0:
            own_side(2)
            own_side(3)
        pick(rep, reps, 0, 384, c, cs, 384, "ofr", 0)
        mm(6, 128, K + (TRS,), ("x1q", "x1s", 0))
        ts(("cap", 0, 64), "kh", "n0", A.subtract, 1e27, A.mult)
        if t == 0:
            memset(("zr", 3, 4), -1e29)
            memset(("zr", 388, 404), 1e29)
            constants_travel()
            dma("y", T.wt[:], T.w[:], [], [whole("wt")])
        else:
            mm(5, 384, ("wq", "ws", 0), (c, cs, 0))
            act(("yw", 0, 384), ("ps", 2560, 2944), F.Copy)
        mm(1, 384, (win, wins, 384), (rep, reps, 0))
        for b in range(3):
            ts(("xk", b, 256, 4), "kr", ("ps", 3152 + b, 3153 + b), A.is_equal, ("lvs", b, b + 1), A.mult)
        quant("xkq", "xks", 0, 128, "xk", 0)
        if t == 0:
            quant(*K, NB, 128, "nb", 0)
            quant("uq", "us", 128, 128, "ut", 512)
        mm(7, 128, ("xkq", "xks", 0), K + (W16,))
        mm(0, 128, ("xkq", "xks", 0), K + (NB,))
        mm(6, 128, K + (WH,), ("xkq", "xks", 0), True, False)
        mm(6, 128, K + (WL,), ("xkq", "xks", 0), False, True)

        def arrived(b):
            if t == 0:
                quant(*K, EB + 128 * b, 128, "eb", 4 - b)
            mm(2 + b, 128, K + (EB + 128 * b,), (win, wins, 384), True, False)

        if t == 1:
            for b in range(4):
                arrived(b)

        def left_side(e):
            act(("af", e, 512, 4), ("ps", 3584, 3712), F.Copy, scale=1024.0)

        scan(("zr", 4, 388), ("ps", 512, 896), "cap", -1e29, A.max, A.min)
        left_side(0)
        left_side(1)
        act("jk", ("zr", 3, 404), F.Sign, bias=("zr", 387, 388), scale=-1.0, acc="ix")
        if t == 0:
            arrived(0)
        runs = ("mk", 0, 12)
        ts(runs, ("zr", 35, 388, 32), ("zr", 387, 388), A.is_lt)
        if t == 0:
            arrived(1)
        red("i32", runs, A.add)
        if t == 0:
            arrived(2)
        ts("gt", "gb", "i32", A.subtract, 32.0, A.mult)
        ts(("xt", 0, 288, 4), "cm", "i32", A.mult, 32.0, A.mult)
        tt("tab", ("ps", 3072, 3136), "kr", A.add)
        if t == 0:
            act("bf", "one", F.Copy, scale=0.0)
        left_side(2)
        left_side(3)
        act("s0", "i32", F.Identity, scale=-32.0, bias="hb")
        act("a32", "i32", F.Copy, scale=32.0)
        act("s2", "ix", F.Identity, scale=-1.0, bias="a32")
        act("ix16", "ix", F.Copy, bias=16.0)
        ts(("xt", 1, 288, 4), "gt", "ix", A.add, -16.0, A.max)
        ts("y1", "ix", 7.5, A.add)
        quant("xtq", "xts", 0, 128, "xt", 0)
        mm(6, 128, K + (TRS,), ("xtq", "xts", 0), True, False)
        mm(6, 128, ("xtq", "xts", 0), K + (NEG,), False, True)
        mm(1, 128, K + (W16,), ("xtq", "xts", 0))
        ts("t16", "y1", 16.0 * C16, A.add, 16.0 * C16 + 16.0, A.subtract)
        if t == 0:
            arrived(3)
        else:
            quant("afq", "afs", 0, 128, "af", 0)
        for e in range(4):
            ts(top(("xm", 96 + e, 608, 4)), top("modb"), top("t16"), A.add, top("ix"), A.is_equal)
        least("nd", ("ps", 3072, 3137))
        ts("oft", ("ps", 580, 584), -1.0, A.add)
        ts(("fm", 0, 256, 4), "tl", "nd", A.is_gt)
        quant("fmq", "fms", 0, 128, "fm", 0)
        for b in (6, 7):
            mm(b, 128, K + (ONES,), ("fmq", "fms", 0))
        for e, x in ((0, "s0"), (1, "vl"), (2, "s2"), (3, -15.0)):
            act(("nm", e, e + 1), "nd", F.Copy, scale=x)
        pick(rep, reps, 0, 64, c, cs, 384, "oft", 0)
        for e in range(4):
            ts(top(("xm", e, 96, 4)), top("kb"), top("t16"), A.is_equal, top(("nm", e, e + 1)), A.mult)
        for b in range(4):
            mm(2 + b, 128, K + (EB + 128 * b,), (rep, reps, 0), False, True)
        act(("jk", 0, 32), ("ps", 3072, 3104), F.Sign, bias="nkh", acc="sa")
        act(("jk", 32, 64), ("ps", 3104, 3136), F.Sign, bias="nkh", acc="sb")
        if t == 0:
            quant("afq", "afs", 0, 128, "af", 0)
        ts("fl", ("ps", 3647, 3648), "p1", A.is_ge)
        mm(7, 128, ("fmq", "fms", 0), K + (ONES,))
        for b in range(4):
            act(("mt", b, 256, 4), ("ps", 512 * (2 + b), 512 * (2 + b) + 64), F.Copy)
        act("qa", "nd", F.Copy, scale="ix16", bias=-1.0)
        act("qb", "nd", F.Copy, scale=1024.0, bias=-1024.0)
        quant("xmq", "xms", 0, 152, "xm", 0)
        mm(1, 128, ("xmq", "xms", 24), ("xmq", "xms", 0), True, False)
        run("v", lambda: g.vector.tensor_scalar(T.bf[:, 0:96:2], T.ps[:, 0:48], T.fl[:], None, A.mult),
            [("ps", 0, 48), whole("fl")], [("bf", 0, 96, 4), ("bf", 2, 96, 4)])
        ts(("bf", 1, 96, 4), ("ps", 48, 72), "sa", A.mult, "fl", A.mult)
        ts(("bf", 3, 96, 4), ("ps", 48, 72), "sb", A.mult, "fl", A.mult)
        quant("bfq", "bfs", 0, 128, "bf", 0)
        mm(1, 128, ("afq", "afs", 0), ("bfq", "bfs", 0), False, True)
        ts("xx", "tab", ("ps", 3584, 3585), A.subtract, 1.0, A.add)
        quant(win, wins, 448, 128, "mt", 0)
        least("pl", "xx")
        cp("ofs", ("ps", 512, 536))
        ts(("tgs", t, t + 1), "pl", "qb", A.mult, "qa", A.add)
        if t == 0:
            dma("y", T.tg[0, :], T.tgs[0:64, 0:1], [("tgs", 0, 1)], [])
            for b in range(3):
                pick(nc, ncs, 128 * b, 128, win, wins, 512, "ofs", 8 * b)
                scores(1, b)
        else:
            mm(2, 128, ("wq", "ws", 0), (win, wins, 384))
            act(("yw", 384, 512), ("ps", 1024, 1152), F.Copy)
            pick_rows(ncs, 0, 192, wins, 512, "ofs", 0)
            pick_rows("ysb", 192, 192, "yw", 512, "ofs", 12)
            pick_rows(ncs, 192, 192, wins, 512, "ofs", 12)
            for b in range(2):
                pick_codes(nc, 192 * b, 192, win, 512, "ofs", 12 * b)
                dma("y", T.oc[:, 768 * b:768 * b + 768], T[nc][:, 192 * b:192 * b + 192].bitcast(dt.uint8),
                    [(nc, 192 * b, 192 * b + 192)], [])
                if b == 0:
                    dma("y", T.tg[1, :], T.tgs[0:64, 1:2], [("tgs", 1, 2)], [])
                    dma("y", T.y[:, 192:384], T.ysb[:, 192:384], [("ysb", 192, 384)], [])
            run("v", lambda: g.vector.tensor_copy(T.ysb[:, 0:192], T.yw[:].indirect(T.ofs[:, 0:12])),
                [whole("yw"), ("ofs", 0, 12)], [("ysb", 0, 192)])
            for k in range(4):
                dma("s", T.osc[4 * k:4 * k + 4, :], T[ncs][32 * k:32 * k + 4, 0:384], [whole(ncs)], [])
            dma("y", T.y[:, 0:192], T.ysb[:, 0:192], [("ysb", 0, 192)], [])
    for s in SEMAPHORES:
        if count[s]:
            g.wait_ge(T.sem[s], count[s])
